import numpy as np, ml_dtypes
CORES = [242,247,114,119]
N = 4
BF = ml_dtypes.bfloat16
def gentries(a):
    return np.ascontiguousarray(a.reshape(8, 16, -1).transpose(0, 2, 1)).reshape(8, -1)
def gtable(e):
    e = np.asarray(e); return np.ascontiguousarray(e.reshape(8, -1, 16).transpose(0, 2, 1)).reshape(128, -1).astype(np.int32)
V, B, L = 1536, 128, 2
W = V + (N - 1) * B
def parts(rng):
    x = (3 * rng.integers(0, 256, (N, 8, 1, V)) + rng.integers(0, 256, (N, 8, 16, V)) + rng.integers(0, 2, (N, 8, 16, V))) >> 2
    t = rng.integers(1, 97, (N, 8, 16, 1)); nx = np.argsort(rng.random((N, 8, 2 * W)), axis=-1)
    sh = np.argsort(rng.random((N, 8, N - 1, V)), axis=-1)[..., :B]
    return np.minimum(x, 255), t, np.ascontiguousarray(nx), np.ascontiguousarray(sh)
def both(rng, a):
    w = rng.integers(0, 2, (len(a), 1)); return 2 * a[:, None] + np.concatenate([w, 1 - w], axis=1)
def chains(rng, g, x, t, nx, sh):
    K = min(B, (V - B) // (3 * N) // 32 * 32); n = N * K
    t[:, g] = 256 * (N - 1) + 1; o = np.argsort(rng.random((N, N - 1, B)), axis=2)
    s = np.stack([3 * n + rng.permutation(V - 3 * n)[:B] for q in range(N)])
    for q in range(N):
        sh[q, g] = s[q][o[q]]
    for r in range(N):
        u = np.concatenate([s[r, :K]] + [V + (d - 1) * B + np.flatnonzero(o[(r - d) % N, d - 1] < K) for d in range(1, N)])
        m = rng.permutation(2 * n); a = m[:n]; e = m[n:]; b = 2 * n + rng.permutation(n)
        x[r, g][:, m] = 0; x[r, g][:, b] = 255; x[r, g][:, s[r, :K]] = 255
        nx[r, g] = np.arange(2 * W)
        for i, j in ((u, a), (a, b), (b, e), (e, u)):
            w = rng.integers(0, 2, n); nx[r, g, 2 * i] = 2 * j + w; nx[r, g, 2 * i + 1] = 2 * j + 1 - w
def put(rng, y, p, nodes, order, high):
    v = rng.integers(0, 4, (4, len(nodes))); y[:, nodes] = order; y[np.ix_(p, nodes)] = 255 - v if high else v
def swell(rng, g, x, t, nx, sh):
    K = 32; n = N * K; m = N * 8; lo = 4 * n
    p = rng.permutation(16)[:4]; t[:, g, p[:2]] = 4095; t[:, g, p[2]] = 0; t[:, g, p[3]] = 301
    o = np.argsort(rng.random((N, N - 1, B)), axis=2); s = np.stack([lo + rng.permutation(V - lo)[:B] for q in range(N)]); one = int(rng.integers(0, N))
    for q in range(N):
        sh[q, g] = s[q][o[q]]
    for r in range(N):
        u = rng.permutation(np.concatenate([s[r, :K]] + [V + (d - 1) * B + np.flatnonzero(o[(r - d) % N, d - 1] < K) for d in range(1, N)]))
        w = rng.permutation(lo); v = x[r, g]; y = nx[r, g]; y[:] = np.arange(2 * W); put(rng, v, p, s[r, :K], 0, True)
        if r != one:
            a = w[:n]; e = w[n:2 * n]; b = w[2 * n:3 * n]
            put(rng, v, p, w[:2 * n], 127, False); put(rng, v, p, b, 254, True)
            for i, j in ((u, a), (a, b), (b, e), (e, u)):
                y[both(rng, i)] = both(rng, j)
        else:
            c = w[:m]; zh = w[m:2 * m]; zl = w[2 * m:3 * m]; f1 = w[3 * m:5 * m]; f2 = w[5 * m:7 * m]; a1 = w[7 * m:10 * m]; a2 = w[10 * m:13 * m]; b = w[13 * m:16 * m]
            for i, k, h in ((c, 254, True), (zh, 254, False), (zl, 0, False), (f1, 127, True), (f2, 127, True), (a1, 127, False), (a2, 127, False), (b, 254, True)):
                put(rng, v, p, i, k, h)
            ui = both(rng, u); uo = both(rng, u)
            i = both(rng, f1); j = both(rng, f1)
            y[both(rng, c).ravel()] = i[:, 0]; y[both(rng, zh).ravel()] = i[:, 1]; y[j[:, 0]] = ui[:2 * m, 0]; y[j[:, 1]] = both(rng, zl).ravel()
            i = both(rng, f2); j = both(rng, f2)
            y[uo[2 * m:, 0]] = i[:, 0]; y[both(rng, zl).ravel()] = i[:, 1]; y[j[:, 0]] = both(rng, c).ravel(); y[j[:, 1]] = both(rng, zh).ravel()
            i = np.concatenate([ui[:2 * m, 1], ui[2 * m:].ravel()]); j = np.concatenate([uo[:2 * m].ravel(), uo[2 * m:, 1]])
            y[both(rng, b).ravel()] = rng.permutation(both(rng, a1).ravel()); y[both(rng, a1).ravel()] = rng.permutation(i)
            y[j] = rng.permutation(both(rng, a2).ravel()); y[both(rng, a2).ravel()] = rng.permutation(both(rng, b).ravel())
def crowd(rng, g, x, nx, sh, two):
    k = W // 5 if two else W // 2; lo = 3 * k if two else k
    x[:, g] = rng.integers(0, 256, (16, 1))
    for q in range(N):
        s = lo + rng.permutation(V - lo)[:B]; y = nx[q, g]; y[:] = np.arange(2 * W)
        for d in range(N - 1): sh[q, g, d] = rng.permutation(s)
        if two:
            ab = k + rng.permutation(2 * k); ce = 3 * k + rng.permutation(2 * k); five = (rng.permutation(k), ab[:k], ab[k:], ce[:k], ce[k:])
            om, oa, ob, oc, oe = [both(rng, z) for z in five]; im, ia, ib, ic, ie = [both(rng, z) for z in five]
            y[oa[:, 0]] = im[:, 0]; y[oa[:, 1]] = ic[:, 1]; y[ob[:, 0]] = im[:, 1]; y[ob[:, 1]] = ie[:, 1]; y[om[:, 0]] = ic[:, 0]; y[om[:, 1]] = ie[:, 0]
            y[oc[:, 0]] = ia[:, 0]; y[oc[:, 1]] = ib[:, 0]; y[oe[:, 0]] = ia[:, 1]; y[oe[:, 1]] = ib[:, 1]
        else:
            a = rng.permutation(k); b = k + rng.permutation(k)
            y[both(rng, a)] = both(rng, b); y[both(rng, b)] = both(rng, a)
def pack(x, t, nx, sh):
    return {"x0": np.ascontiguousarray(x.reshape(N, 128, V)).astype(np.int32), "th": np.ascontiguousarray(t.reshape(N, 128, 1)).astype(np.int32),
            "nxt": np.stack([gtable(a) for a in nx]), "shw": np.stack([gtable(a.reshape(8, -1)) for a in sh])}
def setup_inputs(rng):
    return pack(*parts(rng))
def setup_inputs_flat(rng):
    x, t, nx, sh = parts(rng)
    x[:, 0] = 255; x[:, 2] = rng.integers(0, 2, (N, 16, V)); x[:, 3] = 255 * rng.integers(0, 2, (N, 16, V))
    x[:, 4] = 255 * rng.integers(0, 2, (N, 1, V)); x[:, 5] = rng.integers(0, 4, (N, 1, V)); x[:, 6] = 64 * rng.integers(0, 4, (N, 16, V))
    v = np.array([0, 1, 2, 63, 64, 65, 127, 128, 129, 191, 192, 255, 256])
    t[:, ::2] = rng.choice(v, (N, 4, 16, 1)); t[:, 3] = rng.choice(v, (N, 16, 1)); t[:, 5] = rng.choice(np.array([0, 1, 2, 3]), (N, 16, 1))
    crowd(rng, 1, x, nx, sh, True); crowd(rng, 7, x, nx, sh, False)
    return pack(x, t, nx, sh)
def setup_inputs_loops(rng):
    x, t, nx, sh = parts(rng); p = np.arange(2 * W)
    for q in range(N):
        nx[q, 1] = p; nx[q, 2] = (p ^ 2) ^ np.repeat(rng.integers(0, 2, W), 2)
        nx[q, 3] = (p + 2) % (2 * W); nx[q, 5] = np.where(p & 1 == 0, (p + 2) % (2 * W), (p - 2) % (2 * W))
        i = np.flatnonzero(rng.random(2 * W) < 0.5); nx[q, 6] = p; nx[q, 6, i] = rng.permutation(i)
    chains(rng, 0, x, t, nx, sh); chains(rng, 4, x, t, nx, sh); swell(rng, 7, x, t, nx, sh)
    return pack(x, t, nx, sh)
def setup_inputs_ends(rng):
    x, t, nx, sh = parts(rng); k = 2 * (N - 1) * B
    for q in range(N):
        for g in range(8):
            if g % 2 == 0:
                s = np.concatenate([np.array([0, V - 1]), 1 + rng.permutation(V - 2)[:B - 2]])
                for d in range(N - 1): sh[q, g, d] = rng.permutation(s)
            else:
                sh[q, g] = V - 1 - np.arange((N - 1) * B).reshape(N - 1, B)
            if g in (0, 3, 4):
                o = rng.permutation(2 * V); nx[q, g, 2 * V:] = o[:k]
                nx[q, g, :2 * V] = rng.permutation(np.concatenate([o[k:], np.arange(2 * V, 2 * W)]))
            if g == 5:
                nx[q, g] = np.concatenate([rng.permutation(2 * V), 2 * V + rng.permutation(k)])
    return pack(x, t, nx, sh)
def setup_inputs_uneven(rng):
    x, t, nx, sh = parts(rng); q = rng.permutation(N)
    x[q[0]] = rng.integers(0, 4, (8, 16, V)); t[q[1]] = 4095; t[q[2]] = 0; x[q[3]] = 255 * rng.integers(0, 2, (8, 16, V))
    return pack(x, t, nx, sh)
def setup_inputs_spread(rng):
    x, t, nx, sh = parts(rng)
    x = np.minimum((np.exp2(8 * rng.random((N, 8, 1, V))) * rng.random((N, 8, 16, V))).astype(np.int64), 255)
    t = np.minimum(np.exp2(12 * rng.random((N, 8, 16, 1))).astype(np.int64) - 1, 4095)
    return pack(x, t, nx, sh)
def check_inputs(d):
    bad = []
    for k, lo, hi in (("x0", 0, 255), ("th", 0, 4095), ("nxt", 0, 2 * W - 1), ("shw", 0, V - 1)):
        if np.min(d[k]) < lo or np.max(d[k]) > hi: bad.append("range of " + k)
    if any(np.any(np.sort(gentries(a), axis=1) != np.arange(2 * W)) for a in d["nxt"]): bad.append("nxt holds each number once")
    s = np.sort(np.stack([gentries(a) for a in d["shw"]]).reshape(N, 8, N - 1, B), axis=3)
    if np.any(s[..., 1:] == s[..., :-1]): bad.append("different nodes in a block of shw")
    return bad
def reference(x0, th, nxt, shw):
    x = np.zeros((N, 8, 16, W), np.int32); x[..., :V] = x0.reshape(N, 8, 16, V); t = th.astype(np.int32).reshape(N, 8, 16, 1)
    nx = np.stack([gentries(a) for a in nxt]).astype(np.int64); pv = np.argsort(nx, axis=2)
    sh = np.stack([gentries(a) for a in shw]).astype(np.int64).reshape(N, 8, N - 1, B)
    border = np.zeros((N, 8, V), bool); np.put_along_axis(border, sh.reshape(N, 8, -1), True, 2)
    may = np.zeros((N, 8, W), bool); may[..., :V] = ~border
    inn = np.ones((N, 8, W), bool); port = np.arange(2 * W)
    def pick(a, ports):
        return np.take_along_axis(a, (ports >> 1)[:, :, None, :], 3)
    def sum4(a, n, p):
        b = pick(a, p) + pick(a, n); return b[..., 0::2] + b[..., 1::2]
    def size(u):
        return np.add.reduce(np.minimum(np.abs(u), 255), axis=2)
    def outward(a):
        for r in range(N):
            for d in range(1, N):
                q = (r - d) % N
                a[r, :, :, V + (d - 1) * B:V + d * B] = np.take_along_axis(a[q], sh[q, :, d - 1][:, None, :], 2)
    def home(s):
        o = s[..., :V].copy()
        for r in range(N):
            for d in range(1, N):
                q = (r - d) % N; ix = sh[q, :, d - 1][:, None, :]
                np.put_along_axis(o[q], ix, np.take_along_axis(o[q], ix, 2) + s[r, :, :, V + (d - 1) * B:V + d * B], 2)
        return o
    det = np.zeros((N, 8, 16, W), np.int32); kept = []
    for lev in range(L):
        outward(x)
        a = pick(x, pv); b = pick(x, nx); a0, a1, b0, b1 = a[..., 0::2], a[..., 1::2], b[..., 0::2], b[..., 1::2]
        d = x - ((a0 + a1 + b0 + b1) >> 2)
        key = size(d).astype(np.int64) * 4096 + np.arange(W)
        k = np.minimum(np.take_along_axis(key, pv >> 1, 2), np.take_along_axis(key, nx >> 1, 2))
        lv = may & (key < np.minimum(k[..., 0::2], k[..., 1::2]))
        c = size(a0 - b1) + size(a1 - b0) < size(a0 - b0) + size(a1 - b1)
        s = np.where(lv[:, :, None, :], d >> 2, 0).astype(np.int32)
        x[..., :V] += home(sum4(s, nx, pv)) * inn[:, :, None, :V]
        det = np.where(lv[:, :, None, :], d, det); kept.append((lv, nx, pv, inn))
        l2 = np.repeat(lv, 2, axis=2); other = port ^ np.repeat(c, 2, axis=2).astype(np.int64)
        fn = np.where(l2, np.take_along_axis(nx, other, 2), port); fp = np.where(l2, np.take_along_axis(pv, other, 2), port)
        nx = np.take_along_axis(fn, nx, 2); pv = np.take_along_axis(fp, pv, 2)
        may = may & ~lv; inn = inn & ~lv
    det = np.where(np.abs(det) < t, 0, det).astype(np.int32)
    for lv, n, p, was in kept[::-1]:
        s = np.where(lv[:, :, None, :], det >> 2, 0).astype(np.int32)
        x[..., :V] -= home(sum4(s, n, p)) * was[:, :, None, :V]
        outward(x)
        x = np.where(lv[:, :, None, :], det + (sum4(x, n, p) >> 2), x).astype(np.int32)
    return {"yx": np.ascontiguousarray(x[..., :V]).reshape(N, 128, V).astype(np.float32), "yn": nx.astype(np.float32)}

@@ -1,0 +1,559 @@
+from concourse.bass import DstId, RemoteDMATransfer
+from concourse.mybir import AluOpType, ActivationFunctionType
+
+ALU = AluOpType
+FN = ActivationFunctionType
+V, W, GH, NB, LW = 1536, 1920, 384, 128, 120
+MAGIC = 12582912.0
+OWN = [(0, 512), (512, 1024), (1024, V)]
+CFG = {
+    "na": 1760, "piece": 608,
+    "xp": [(V, W), (0, 1024), (1024, V)], "xc": [(V, W)] + OWN, "kp": OWN, "ec": OWN + [(V, W)], "lp": [(0, 960), (960, W)],
+    "s1": [(V, W, "mix"), (0, 512, "pe"), (512, 1024, "mix"), (1024, V, "mix")],
+    "s2": [(V, W, "pe"), (0, 512, "pe"), (512, 1024, "mix"), (1024, V, "mix")],
+    "u2": [(0, 512, "dbl"), (512, 1024, "mix"), (1024, 1280, "mix"), (1280, V, "mix")],
+    "u1": [(0, 512, "dbl"), (512, 1024, "mix"), (1024, 1280, "mix"), (1280, V, "mix")],
+    "flip": (0, 2),
+    "banks": {"D": [6, 7], "y": [5, 6, 7], "e": [0, 1, 2], "u": [3, 4], "kp": [0, 6], "za": [1, 7], "m": [2], "f": [5], "sm": [0, 1],
+              "kl": [2, 0, 1], "xh": [3, 4, 2, 0], "um": [0, 1, 2]},
+}
+QUEUE = "asssvvaagaavggvvaavvvggvvvvvvvvvvggggggggvagggggggggggggggggggggggggggvavvvvvgxvapvaaavvvvssppavppavaavpvvvvvvvaaavaaavapppvappvpppvappapppvappapppvappvpvpapvpapapapapapapapapaavvvavvvavvvapvppappvapvppappvapvppappvppppvpavpvvvvvppvvvvsvvsaavvvgxaaaappppaavvvavvvpvpvpvvvvvvvvgxaapvvaapvaaapavaapavvppvvppvvppvvppvvaavvvvavvaapppvavppvpppvavppapppvavppvpppvavppvpaapaapaapavpavpavpaapaapaapavpavpavvvvvavvvavvvapvppappvapvppappvapvppappvppppvpavpvvvvvpvvvsaaaaappppagxaaaappppvvvvvvvvvpvpvpvvvvvvvagxvpvaavaspaaavvppaavvvppavvvvppaavvvppaaavvppasavvvppasavvvppasvvvvppas"
+ORDER = "0002050l01030w0r06070u0t0s040n0q080o0p0v0a0d0j0b0g1d0h0c0f0k091c1h1i0O0i1j0e0x1k0m1m1o1e0J1p1f1n1q0y1g0z1u0M1r0A1l1t0S1v1y1w1z1s1A1x0K1O1L0L1P1K0T24291B1N0N1E1D1W1M1C0B2h1R0V1F1G1Q0Q2c1U1T1X2u0U1S251Y0W2d2v1Z262717202k0C1V1H2e0R2s2f282l0D2t2m2g0P212n2a223e232o0E2i1I102p2b2q180F2w2j2r1135192x2Q2y1J2A0Y0G2R332B2U142S2E3c2z2V0X2F2C2T0Z3t2D2W2Y152G342I2H2Z12362J3l2X37162K3230382L133d393b2O313k2M0H3a3f0I3n3g3m3h2N1a3y2P1b3i3z3o3j3B3p3q3C3D3r3E3u3s3F3S3G3v473T3w3Y48403H3x3I4f3A4b3J4j3K3U423Z3L3M3N3O41433P443V3Q454c3W463X493R4h4a4u4d4e4v4l4m4K4w4n4o4p4E4q4r4P4O4J4s4T4g4t4S4X4z4W4x4i4Q4y4Y4A4R4U4Z51504F4V524B5354554G4k4C584D4H4L5b844I5m595y4M5p5e575E4N5z5d5g5q5a565A5c5h5i5f5r5v5j5B5k5H5s5C5I5J5l5t5K5n5Q5o5L5D5N6U5u5F5M5w5G5O5x5T5P6L6M6q6u6O6r5U6F5R5Z6s6D606v6y5W6t6C656E666w5X6V5Y6x6G6b6H6z6I6c6N6J5S6X6A6P626Q6K636B6R5V6S6d6W686T6Y6Z6770616964716h727b7q7L737n7H7o7r7M7p7s7y7N7t7u7I7v7C7z7w7T7J7x7A7D6e7O7B7E7P7K6i7F747G6f6a7V6k7W6g6n7X7Y786o7Z6l807R797c75817d7e7U827f837g7h7Q7m7S6m8p6j6p768s8z8e8A8c8B8f8g8l8C8i8h8d8m8j8n8w8k8t8o8D8E8u8q8F8v778x7a8r7i908y7j857k8G8S947l868O8I8H958K8P8W878J8Q8L888R8X8T8a8Y968Z978M91898U8N9899928V939a8b9b"
+I32, U16, F32, F16, B16 = "int32", "uint16", "float32", "float16", "bfloat16"
+SB = {}
+for _d, _l in ((I32, "nxi:240 shi:24 thi:4 xi:1920 d32:1920 s32:1536 s0:384 pi:240 pc:4 pd:4"),
+               (U16, "shu:24 praw:240 nd1:480 nd2:480 ps1:480 ps2:240 ul1:480 ul2:480"),
+               (F32, "thb:4 xw2:1920 kw:1920 t:1536 pk:1920 hh:1920 hg1:384 hg2:384 rc1:384 rc2:384 tm:384 s1:384 s2:384 w2:1920 "
+                     "z1:3840 z2:3840 lw:3840 iv:1792 zc:240 c1:240 c2:240 idf:480 pf:4 lvs:120 cc:120 lc:120 t1:480 ff:480 f1:128 fq:128 f2k:128"),
+               (F16, "ab:7680 gg:7680 ad:1920 adc:1920 lv1:1536 lv2:1536 sg:1536 rr:6144 h1:1536 h2:1536 r16:1920 qc:240 br:240 b16:480 "
+                     "pr16:240 q1:480 q2:480 id16:480 im257:128 ibeta:128 im2047:128"),
+               (B16, "nomay:1536 nb:1920 big:128 ones:512 zb:128 crow:384 nw:128 gs:128 gt:144 bt:144 bf:144 bfn:144 bfs:144 bp0:144 bp1:144 "
+                     "di:512 i1:128 im1:128 imq:128 imh:128 i4k:128 im120:128 ieps:128")):
+    for _x in _l.split():
+        SB[_x.split(":")[0]] = (int(_x.split(":")[1]), _d)
+SCALED = {"im1": -1.0, "imq": -0.25, "imh": -0.5, "i4k": 4096.0, "im120": -120.0, "ieps": 1.0 / 2048, "im257": -257.0,
+          "ibeta": 2047.0 / 4096, "im2047": -2047.0, "f1": 1.0, "fq": 0.25, "f2k": 2048.0}
+SCRATCH = {k: ("sbuf", [128, n], d) for k, (n, d) in SB.items()}
+for _k in range(8):
+    SCRATCH["bank%d" % _k] = ("psum", [128, 512], F32)
+SEMAPHORES = ["ev", "ea", "ep", "eg", "loc"] + ["ar%d" % k for k in range(5)] + ["dm%d" % k for k in range(16)]
+
+
+def S(buf, lo, hi, step=1, p=None):
+    return (buf, lo, hi, step, p)
+
+
+def width(r):
+    return (r[2] - r[1] + r[3] - 1) // r[3]
+
+
+def psum(r):
+    return r[0][0] == "#"
+
+
+def two(r):
+    return (not psum(r)) and SB[r[0]][1] in (F16, B16, U16)
+
+
+def ap(T, r):
+    if isinstance(r, (int, float)):
+        return r
+    t = T["bank" + r[0][1:]] if psum(r) else T[r[0]]
+    p = slice(0, 128) if r[4] is None else slice(r[4][0], r[4][1], r[4][2])
+    return t[p, r[1]:r[2]] if r[3] == 1 else t[p, r[1]:r[2]:r[3]]
+
+
+def build(C):
+    ops, acc, ntile, ndma = [], {}, {}, [0]
+
+    def meet(a, b):
+        if a[1] >= b[2] or b[1] >= a[2]:
+            return False
+        return a[4] is None or b[4] is None or len(set(range(*a[4])) & set(range(*b[4]))) > 0
+
+    def add(name, impl, reads, writes, **kw):
+        k, deps = len(ops), set()
+        for r, wr in [(r, False) for r in reads if isinstance(r, tuple)] + [(r, True) for r in writes]:
+            for (j, q, wq) in acc.get(r[0], [])[-12 if psum(r) else 0:]:
+                if j != k and (psum(r) or ((wr or wq) and meet(r, q))):
+                    deps.add(j)
+            acc.setdefault(r[0], []).append((k, r, wr))
+        ops.append(dict(kw, name=name, impl=impl, deps=deps))
+        return k
+
+    def tile(pool, m):
+        banks = C["banks"][pool]
+        ntile[pool] = ntile.get(pool, -1) + 1
+        return S("#%d" % banks[ntile[pool] % len(banks)], 0, m)
+
+    def vts(o, i, s1, s2, op0, op1=None):
+        n = width(i) * (0.5 if two(o) and two(i) else 1)
+        if op1 is None:
+            return ("v", n, lambda q, T: q.tensor_scalar(ap(T, o), ap(T, i), ap(T, s1), None, op0))
+        return ("v", n, lambda q, T: q.tensor_scalar(ap(T, o), ap(T, i), s1, s2, op0, op1))
+
+    def aact(o, i, f, bias, scale):
+        return ("a", width(i), lambda q, T: q.activation(ap(T, o), ap(T, i), f, bias=ap(T, bias), scale=scale))
+
+    def ts(name, o, i, s1, s2, op0, op1=None):
+        add(name, {"v": vts(o, i, s1, s2, op0, op1)}, [i, s1], [o])
+
+    def act(name, o, i, f, bias=0.0, scale=1.0):
+        add(name, {"a": aact(o, i, f, bias, scale)}, [i, bias], [o])
+
+    def lin(name, o, i, scale, bias):
+        add(name, {"v": vts(o, i, scale, bias, ALU.mult, ALU.add), "a": aact(o, i, FN.Identity, bias, scale)}, [i], [o])
+
+    def tt(name, o, a, b, op):
+        n = width(a) * (1 if psum(a) or psum(b) else 2)
+        add(name, {"v": ("v", n, lambda q, T: q.tensor_tensor(ap(T, o), ap(T, a), ap(T, b), op))}, [a, b], [o])
+
+    def ind(T, win, idx):
+        return ap(T, win).indirect(ap(T, idx))
+
+    def gat(name, o, win, idx, bias=0.0):
+        def fv(q, T):
+            if bias == 0.0:
+                return q.tensor_copy(ap(T, o), ind(T, win, idx))
+            return q.tensor_scalar(ap(T, o), ind(T, win, idx), bias, None, ALU.add)
+        add(name, {"v": ("vg", width(o), fv),
+                   "a": ("ag", width(o), lambda q, T: q.activation(ap(T, o), ind(T, win, idx), FN.Identity, bias=bias, scale=1.0))}, [win, idx], [o])
+
+    def gop(name, o, win, idx, b, op):
+        add(name, {"v": ("vg", width(o), lambda q, T: q.tensor_tensor(ap(T, o), ind(T, win, idx), ap(T, b), op))}, [win, idx, b], [o])
+
+    def sca(name, win, idx, i):
+        add(name, {"v": ("vs", width(i), lambda q, T: q.tensor_copy(ind(T, win, idx), ap(T, i)))}, [idx, i], [win])
+
+    def mm(name, o, terms, start=True, stop=True):
+        cyc = sum(max(64, width(r)) * (4 if SB[r[0]][1] == F32 else 1) for l, r in terms)
+
+        def f(q, T):
+            ins = None
+            for k, (l, r) in enumerate(terms):
+                ins = q.matmul(ap(T, o), ap(T, l), ap(T, r), start and k == 0, stop and k == len(terms) - 1)
+            return ins
+        add(name, {"p": ("p", (cyc, len(terms)), f)}, [x for lr in terms for x in lr], [o])
+
+    def I(name):
+        return S(name, 0, 128)
+
+    def cst(k, n):
+        return (S("crow", 128 * k, 128 * k + 128, 1, (0, 1, 1)), S("ones", 0, n, 1, (0, 1, 1)))
+
+    def fill(name, o, c):
+        add(name, {"v": ("v", width(o) * (0.5 if two(o) else 1), lambda q, T: q.memset(ap(T, o), c))}, [], [o])
+
+    def iota(name, o, pat, base, cm):
+        kw = {} if SB[o[0]][1] == I32 else {"allow_small_or_imprecise_dtypes": True}
+        add(name, {"g": ("g", width(o), lambda q, T: q.iota(ap(T, o), pat, base, cm, **kw))}, [], [o])
+
+    def gsel(o, i, pat, op, fl, base, cm):
+        return ("g", width(o), lambda q, T: q.affine_select(ap(T, o), ap(T, i), pat, op, fl, base, cm))
+
+    def sel(name, n, src, pat, op, base, cm, lo=0):
+        o, i = S(name, lo, lo + n), S(src, 0, n)
+        add(name, {"g": gsel(o, i, pat, op, 0.0, base, cm)}, [i], [o])
+
+    def dma(name, o, i, nbytes, eng="s"):
+        out = o[0] in ("yx", "yn")
+        ndma[0] += 1
+
+        def f(q, T):
+            dst = ap(T, o) if not out else (T[o[0]][:, o[1]:o[2]] if o[2] else T[o[0]][:])
+            return q.dma_start(dst, T[i][:] if isinstance(i, str) else ap(T, i))
+        add(name, {eng: ("dma", nbytes, f)}, [i], [] if out else [o], sem="dm%d" % (ndma[0] - 1), final=out)
+
+    def exchange(k, src, dst, off, sign):
+        s = add("send%d" % k, {"g": ("rem", 1 if k == 0 else 0, (k, src, dst, off, sign))}, [S(src, 0, GH)], [], send=True)
+        a = add("arrive%d" % k, {"x": ("arr", 0, None)}, [], [S(dst, off, off + GH)], sem="ar%d" % k)
+        ops[a]["deps"].add(s)
+
+    def lst(buf, j, lo=0, hi=W):
+        return S(buf, LW * j + lo // 16, LW * j + hi // 16)
+
+    def row(buf, r=0):
+        return S(buf, 0, 2 * W, 1, (r, 128, 16))
+
+    def squeeze(name, o, mask, buf, lo, n, start=True, stop=True):
+        mm(name, o, [(S(mask, 15 - i, 143 - i), S(buf, lo + i, lo + n, 16)) for i in range(16)], start, stop)
+
+    POSC = 120.0 * 1920 + 3839.0 * 1030
+
+    def positions(name, o, q, b):
+        tl = tile("D", 240)
+        mm(name + "m", tl, [(I("im120"), q), (I("i4k"), b), (I("im257"), b)])
+        lin(name, o, tl, -1.0, POSC)
+        return tl
+
+    RB, SH = 128 * 960, S("shu", 0, 24)
+    dma("ld_nxt", S("nxi", 0, 240), "nxt", RB, "a")
+    dma("ld_shw", S("shi", 0, 24), "shw", 128 * 96)
+    dma("ld_x", S("xi", 0, V), "x0", 128 * V * 4)
+    dma("ld_th", S("thi", 0, 1), "th", 128 * 64)
+    fill("zb", I("zb"), 0.0)
+    fill("zc", S("zc", 0, 240), 0.0)
+    dma("z1row", row("z1"), S("zc", 0, 240), RB, "a")
+    dma("z2row", row("z2"), S("zc", 0, 240), RB, "a")
+    add("i1", {"g": gsel(I("i1"), I("zb"), [[-1, 128]], ALU.not_equal, 1.0, 0, 1)}, [I("zb")], [I("i1")])
+    for k, c in SCALED.items():
+        impl = {"v": vts(I(k), I("i1"), c, None, ALU.mult), "a": aact(I(k), I("i1"), FN.Identity, 0.0, c)}
+        if SB[k][1] == B16:
+            impl["g"] = gsel(I(k), I("zb"), [[-1, 128]], ALU.not_equal, c, 0, 1)
+        add(k, impl, [I("i1"), I("zb")], [I(k)])
+    NA, PC = C["na"], C["piece"]
+    iota("iv0", S("iv", 0, PC), [[1, PC]], 64, 0)
+    iota("iv1", S("iv", PC, NA), [[1, NA - PC]], 64 + PC, 0)
+    fill("ones", S("ones", 0, 512), 1.0)
+    for k, c in enumerate([MAGIC, -MAGIC, 0.375]):
+        fill("crow", cst(k, 1)[0], c)
+    NW = S("nw", 0, 128, 1, (0, 64, 1))
+    fill("nw", NW, 0.0)
+    fill("nw", S("nw", 0, 128, 1, (0, 1, 1)), 1.0 / 2048)
+    fill("nw", S("nw", 0, 128, 1, (32, 33, 1)), 1.0 / 32)
+    fill("big", I("big"), 4096.0)
+    fill("lvs", S("lvs", 96, LW), 0.0)
+    fill("lc", S("lc", 96, LW), 0.0)
+    for k in range(4):
+        sel("di", 128, "ones", [[16, 8], [1000, 2], [2, 8]], ALU.is_equal, k // 2 - 1000 * (k % 2), -1, 128 * k)
+    sel("gt", 128, "ones", [[-16, 8], [0, 16]], ALU.is_ge, 0, 1)
+    sel("gs", 128, "gt", [[16, 8], [0, 16]], ALU.is_ge, 15, -1)
+    sel("bt", 144, "ones", [[16, 9], [1000, 16]], ALU.is_ge, 15 - 15000, -1)
+    sel("bf", 144, "bt", [[-16, 9], [0, 16]], ALU.is_ge, 0, 1)
+    lin("bfn", S("bfn", 0, 144), S("bf", 0, 144), -1.0, 0.0)
+    lin("bfs", S("bfs", 0, 144), S("bf", 0, 144), 1.0 / 16, 0.0)
+    for r in range(2):
+        sel("bp%d" % r, 144, "ones", [[16, 9], [1000, 16]], ALU.is_equal, r - 15000, -1)
+    for lo in range(0, W, 384):
+        iota("nb0", S("nb", lo, lo + 384, 1, (0, 32, 1)), [[0, 6], [1, 64]], 0, 0)
+        iota("nb1", S("nb", lo, lo + 384, 1, (32, 64, 1)), [[1, 6], [0, 64]], lo // 64, 0)
+    for buf, a, b, n in (("nomay", 0, V, 384), ("pk", V, W, 384), ("lw", 0, 2 * W, 480)):
+        for lo in range(a, b, n):
+            iota("z" + buf, S(buf, lo, lo + n), [[0, n]], 0, 0)
+    ID = S("idf", 0, 480)
+    iota("idi", ID, [[0, 2], [1, 2], [32, LW]], 0, 0)
+    iota("pc", S("pc", 0, 1), [[0, 1]], 0, 2)
+    ts("pd", S("pd", 0, 1), S("pc", 0, 1), 31, None, ALU.bitwise_and)
+    lin("pf", S("pf", 0, 1), S("pd", 0, 1), 1.0, 0.0)
+    ts("idf", ID, ID, S("pf", 0, 1), None, ALU.add)
+    lin("id16", S("id16", 0, 480), ID, 1.0, -1920.0)
+    lin("thb", S("thb", 0, 1), S("thi", 0, 1), -1.0, -4095.5)
+
+    lin("shu", SH, S("shi", 0, 24), 1.0, 0.0)
+    gat("s0", S("s0", 0, GH), S("xi", 0, V), SH)
+    exchange(0, "s0", "xi", V, 1)
+
+    lin("qc", S("qc", 0, 240), S("nxi", 0, 240), 1.0, -1920.0)
+    lin("br", S("br", 0, 240), S("nxi", 0, 240), 1.0 / 32, 1030 - 31.0 / 64)
+    tl = positions("praw", S("praw", 0, 240), S("qc", 0, 240), S("br", 0, 240))
+    lin("pr16", S("pr16", 0, 240), tl, -1.0, POSC - 1920)
+
+    def scatter(eng, lo, hi):
+        idx = S("praw", lo // 16, hi // 16)
+        if eng == "a":
+            z, i = S("z2", 0, 2 * W), S("iv", lo, hi)
+            add("sca", {"a": ("as1" if lo == 0 else "as", hi - lo, lambda q, T: q.activation(ind(T, z, idx), ap(T, i), FN.Silu))}, [idx, i], [z])
+        else:
+            z, i = S("z1", 0, 2 * W), S("iv", 0, hi - lo)
+            add("scv", {"v": ("vs", hi - lo, lambda q, T: q.tensor_scalar(ind(T, z, idx), ap(T, i), 1.0, float(lo), ALU.mult, ALU.add))}, [idx, i], [z])
+    scatter("a", 0, PC)
+    scatter("a", PC, NA)
+    for lo in range(NA, 2 * W, PC):
+        scatter("v", lo, min(lo + PC, 2 * W))
+    dma("c1", S("c1", 0, 240), row("z1"), RB)
+    dma("c2", S("c2", 0, 240), row("z2"), RB)
+    for src in ("qc", "pr16"):
+        tl = tile("D", 240)
+        for j in range(2):
+            mm("dei", lst(tl[0], j), [(S("di", 128 * (2 * j + h), 128 * (2 * j + h) + 128), S(src, h, 240, 2)) for h in range(2)])
+        if src == "qc":
+            lin("nd1n", S("nd1", 240, 480), tl, 0.5, 959.75)
+            lin("q1n", S("q1", 240, 480), tl, 1.0, 0.0)
+        else:
+            lin("ps1n", S("ps1", 240, 480), tl, 1.0, 1920.0)
+    PI = S("pi", 0, 240)
+    tt("pi", PI, S("c1", 0, 240), S("c2", 0, 240), ALU.add)
+    lin("nd1p", S("nd1", 0, 240), PI, 0.5, -32.25)
+    lin("q1p", S("q1", 0, 240), PI, 1.0, -1984.0)
+    lin("b1p", S("b16", 0, 240), PI, 1.0 / 32, 1028 - 31.0 / 64)
+    positions("ps1p", S("ps1", 0, 240), S("q1", 0, 240), S("b16", 0, 240))
+    for d in range(3):
+        sca("border", S("nomay", 0, V), S("shu", 8 * d, 8 * d + 8), I("big"))
+
+    def level(lev):
+        n = "%d" % lev
+        win, nd, qq, lv, size = ("xi" if lev == 1 else "xw2"), "nd" + n, "q" + n, "lv" + n, ("ad" if lev == 1 else "adc")
+
+        def nbr(j, lo, hi):
+            return S("ab", W * j + lo, W * j + hi)
+
+        def key(lo, hi):
+            return [(NW, S("nb", lo, hi, 1, (0, 64, 1))), (I("gs"), S(size, lo, hi))]
+        for j in (2, 3, 0, 1):
+            for lo, hi in C["xp"]:
+                gat("x" + n, nbr(j, lo, hi), S(win, 0, W), lst(nd, j, lo, hi), -0.375)
+        for lo, hi in C["xc"]:
+            tl, d = tile("y", hi - lo), S("d32", lo, hi)
+            mm("yb" + n, tl, [(I("imq"), nbr(j, lo, hi)) for j in (2, 3)], True, False)
+            mm("ya" + n, tl, [(I("imq"), nbr(0, lo, hi))], False, False)
+            mm("ya" + n, tl, [(I("imq"), nbr(1, lo, hi))], False, True)
+            tt("d" + n, d, tl, S(win, lo, hi), ALU.add)
+            act("ad" + n, S("ad", lo, hi), d, FN.Abs)
+            if lev == 2:
+                ts("adc", S("adc", lo, hi), S("ad", lo, hi), 255.0, None, ALU.min)
+            tl = tile("e", hi - lo)
+            mm("e" + n, tl, key(lo, hi)[:1], True, False)
+            mm("eb" + n, tl, key(lo, hi)[1:], False, True)
+            lin("key" + n, S("kw", lo, hi), tl, 1.0, 0.0)
+        terms = [(0, 2, -1), (1, 3, -1), (0, 3, 1), (1, 2, 1)]
+        for k, (a, b, sgn) in enumerate(terms):
+            for lo, hi in OWN:
+                tl, r = tile("u", hi - lo), S("rr", V * k + lo, V * k + hi)
+                mm("u" + n, tl, [(I("im1"), nbr(b, lo, hi)), (I("i1"), nbr(a, lo, hi))])
+                if lev == 1:
+                    add("r1", {"v": vts(r, tl, 0.0, None, ALU.max), "a": aact(r, tl, FN.Relu, 0.0, 1.0)}, [tl], [r])
+                else:
+                    act("r2", r, tl, FN.Abs)
+                    if k in C["flip"]:
+                        act("r2a", r, r, FN.Relu, 255.0, -1.0)
+                    else:
+                        ts("r2v", r, r, 255.0, None, ALU.min)
+        for lo, hi in C["kp"]:
+            t = S("t", lo, hi)
+            gat("k" + n, t, S("kw", 0, W), lst(nd, 0, lo, hi))
+            for j in (1, 2, 3):
+                gop("kc" + n, t, S("kw", 0, W), lst(nd, j, lo, hi), t, ALU.min)
+        for lo, hi in C["kp"]:
+            m, s, d, l, sg = hi - lo, S("s32", lo, hi), S("d32", lo, hi), S(lv, lo, hi), S("sg", lo, hi)
+            add("s" + n, {"v": vts(s, d, 2, None, ALU.arith_shift_right), "a": aact(s, d, FN.Identity, -0.375, 0.25)}, [d], [s])
+            tl = tile("kp", m)
+            mm("kp" + n, tl, key(lo, hi) + [(I("i1"), S("nomay", lo, hi))] + ([(I("i4k"), S("lv1", lo, hi))] if lev == 2 else []))
+            tt("lv" + n, l, tl, S("t", lo, hi), ALU.is_lt)
+            tl = tile("za", m)
+            mm("za" + n, tl, [(I("i1"), S("ad", lo, hi))], True, False)
+            mm("zb" + n, tl, [(I("i4k"), l)], False, True)
+            act("sg" + n, sg, tl, FN.Sign, S("thb", 0, 1))
+            tl = tile("m", m)
+            a, b = ("ieps", "ibeta") if lev == 1 else ("i1", "imh")
+            mm("m" + n, tl, [(I(b), S("ones", 0, m)), (I(a), l)], True, False)
+            mm("mb" + n, tl, [(I(b), sg)], False, True)
+            tt("pk" + n, S("pk", lo, hi), tl, s, ALU.mult)
+        tf = tile("f", 96)
+        for k, (a, b, sgn) in enumerate(terms):
+            if lev == 2 and k in C["flip"]:
+                sgn = -sgn
+            squeeze("f" + n, tf, "bf" if sgn > 0 else "bfn", "rr", V * k, V, k == 0, k == 3)
+        ts("cc" + n, S("cc", 0, 96), tf, 0.0, None, ALU.is_lt)
+        tl = tile("D", 96)
+        squeeze("lvq" + n, tl, "bfs", lv, 0, V)
+        lin("lvs" + n, S("lvs", 0, 96), tl, 1.0, 0.0)
+        tt("lc" + n, S("lc", 0, 96), S("lvs", 0, 96), S("cc", 0, 96), ALU.mult)
+        td, tx = tile("D", 480), tile("D", 480)
+        mm("d1" + n, td, [(I("i1"), S(qq, 0, 480)), (I("im1"), S("id16", 0, 480))])
+        for j in (2, 3, 0, 1):
+            tt("xa" + n, lst(tx[0], j), lst(td[0], j), S("lvs", 0, LW), ALU.mult)
+        tt("t1" + n, S("t1", 0, 480), tx, ID, ALU.add)
+        td, tx = tile("D", 240), tile("D", 240)
+        sides = (1, 0) if lev == 1 else (1,)
+        for k in sides:
+            mm("d2" + n, lst(td[0], k), [(I("i1"), lst(qq, 2 * k + 1)), (I("im1"), lst(qq, 2 * k))])
+        for k in sides:
+            tt("xb" + n, lst(tx[0], k), lst(td[0], k), S("lc", 0, LW), ALU.mult)
+        for k in sides:
+            tt("f0" + n, lst("ff", 2 * k), lst("t1", 2 * k), lst(tx[0], k), ALU.add)
+            tt("f1" + n, lst("ff", 2 * k + 1), lst("t1", 2 * k + 1), lst(tx[0], k), ALU.subtract)
+            dma("lw" + n, row("lw", 1 - k), S("ff", 240 * k, 240 * k + 240), RB)
+        lin("ul" + n, S("ul" + n, 0, 480), S("t1", 0, 480), 0.5, -0.25)
+        own, hg, PK = ("hh" if lev == 1 else "w2"), "hg" + n, S("pk", 0, W)
+        for lo, hi, mode in C["s" + n]:
+            o = S(hg, lo - V, hi - V) if lo >= V else S(own, lo, hi)
+            plain = lev == 1 or lo >= V
+            if mode == "mix":
+                if plain:
+                    gat("sa" + n, o, PK, lst(nd, 0, lo, hi))
+                else:
+                    gop("sa" + n, o, PK, lst(nd, 0, lo, hi), S("xw2", lo, hi), ALU.add)
+                for j in (1, 2, 3):
+                    gop("sc" + n, o, PK, lst(nd, j, lo, hi), o, ALU.add)
+            else:
+                tl = tile("sm", hi - lo)
+                for j in range(4):
+                    gat("sp" + n, S("gg", W * j + lo, W * j + hi), PK, lst(nd, j, lo, hi))
+                for j in range(4):
+                    mm("sm" + n, tl, [(I("i1"), S("gg", W * j + lo, W * j + hi))], j == 0, j == 3)
+                if plain:
+                    lin("se" + n, o, tl, 1.0, 0.0)
+                else:
+                    tt("se" + n, o, tl, S("xw2", lo, hi), ALU.add)
+            if hi == W:
+                exchange(2 * lev - 1, hg, "rc" + n, 0, -1)
+        for lo, hi in OWN:
+            tl = tile("kl", hi - lo)
+            mm("kl" + n, tl, [(I("imh"), S("ones", 0, hi - lo)), (I("imh"), S("sg", lo, hi))])
+            tt("h" + n, S("h" + n, lo, hi), tl, S("d32", lo, hi), ALU.mult)
+        for d in range(3):
+            blk, tm = S("shu", 8 * d, 8 * d + 8), S("tm", NB * d, NB * d + NB)
+            gop("home" + n, tm, S(own, 0, V), blk, S("rc" + n, NB * d, NB * d + NB), ALU.add)
+            sca("homes" + n, S(own, 0, V), blk, tm)
+        gat("out" + n, S("s" + n, 0, GH), S(own, 0, V), SH)
+        exchange(2 * lev, "s" + n, own, V, 1)
+
+    level(1)
+    for j in (2, 3, 0, 1):
+        for lo, hi in C["lp"]:
+            gat("lk", S("ab", W * j + lo, W * j + hi), S("lw", 0, 2 * W), lst("ps1", j, lo, hi), -1920.0)
+        tl = tile("D", LW)
+        squeeze("lq", tl, "bp0" if j >= 2 else "bp1", "ab", W * j, W)
+        lin("nd2", lst("nd2", j), tl, 0.5, 959.75)
+        lin("q2", lst("q2", j), tl, 1.0, 0.0)
+    for lo, hi in C["ec"]:
+        tl, h, r = tile("xh", hi - lo), S("hh", lo, hi), S("r16", lo, hi)
+        ts("r16", r, h, MAGIC, MAGIC, ALU.add, ALU.subtract)
+        mm("xh", tl, [(I("f2k"), h)], True, False)
+        mm("xr", tl, [(I("im2047"), r), cst(2, hi - lo)], False, True)
+        tt("xw2", S("xw2", lo, hi), tl, S("xi", lo, hi), ALU.add)
+    level(2)
+    lin("b2", S("b16", 240, 480), S("q2", 240, 480), 1.0 / 32, 1090 - 31.0 / 64)
+    positions("ps2", S("ps2", 0, 240), S("q2", 240, 480), S("b16", 240, 480))
+    for j, h in ((0, 0), (1, 1), (1, 0), (0, 1)):
+        lo, hi = 960 * h, 960 * h + 960
+        gat("yn", S("z1", 2 * lo + j, 2 * hi, 2), S("lw", 0, 2 * W), lst("ps2", j, lo, hi))
+    dma("st_yn", ("yn", 0, 0), row("z1"), RB)
+
+    def undo(lev, win, lo, hi, mode):
+        ul, m, t, t2 = "ul%d" % lev, hi - lo, S("t", lo, hi), S("hh", lo, hi)
+        tl, rnd = tile("um", m), ([] if lev == 2 else [cst(0, m), cst(1, m)])
+        gat("ug", t, win, lst(ul, 0, lo, hi), -3.0 if lev == 2 else -1.5)
+        first = [(I("im1"), S("h%d" % lev, lo, hi))] + ([(I("im1"), S("r16", lo, hi))] if lev == 2 else [])
+        if mode == "dbl":
+            gat("ug", t2, win, lst(ul, 1, lo, hi))
+            gop("uc", t, win, lst(ul, 2, lo, hi), t, ALU.add)
+            gop("uc", t2, win, lst(ul, 3, lo, hi), t2, ALU.add)
+            mm("um", tl, first + [(I("fq"), t)], True, False)
+            mm("um", tl, [(I("fq"), t2)] + rnd, False, True)
+        else:
+            for j in (1, 2, 3):
+                gop("uc", t, win, lst(ul, j, lo, hi), t, ALU.add)
+            mm("um", tl, first, True, False)
+            mm("um", tl, [(I("fq"), t)] + rnd, False, True)
+        return tl
+
+    tl = tile("um", GH)
+    mm("wg", tl, [(I("im1"), S("r16", V, W)), (I("f1"), S("w2", V, W))])
+    lin("w1g", S("d32", V, W), tl, 1.0, 0.0)
+    for lo, hi, mode in C["u2"]:
+        lin("w1", S("d32", lo, hi), undo(2, S("w2", 0, W), lo, hi, mode), 1.0, 0.0)
+    for lo, hi, mode in C["u1"]:
+        y = S("z2", 2048 + lo, 2048 + hi)
+        lin("y", y, undo(1, S("d32", 0, W), lo, hi, mode), 1.0, 0.0)
+        dma("st_x", ("yx", lo, hi), y, 512 * (hi - lo))
+    return ops
+
+
+def plan(ops, sc):
+    eng, order = sc["eng"], sc["order"]
+    pos = {k: i for e in order for i, k in enumerate(order[e])}
+    keep, marked, count = {e: [] for e in order}, set(), {}
+    for e in order:
+        seen, prev = {}, None
+        for k in order[e]:
+            last, deps = {}, set(ops[k]["deps"])
+            if e == "g" and not ops[k].get("send"):
+                if prev is not None and "nb1" in (ops[k]["name"], ops[prev]["name"]):
+                    deps.add(prev)
+                prev = k
+            for j in deps:
+                if e == "x" or ops[j].get("send") or (e == "p" and eng[j] == "p"):
+                    continue
+                key = ops[j].get("sem") or eng[j]
+                if pos[j] > seen.get(key, -1) and (key not in last or pos[j] > pos[last[key]]):
+                    last[key] = j
+            for key, j in last.items():
+                seen[key] = pos[j]
+                marked.add(j)
+            keep[e].append((k, sorted(last.values())))
+    for e in order:
+        c = 0
+        for k in order[e]:
+            if ops[k].get("sem"):
+                count[k] = (ops[k]["sem"], 16)
+            elif k in marked:
+                c += 1
+                count[k] = ("e" + e, c)
+    return keep, count
+
+
+CACHE = {}
+DIGITS = "0123456789abcdefghijklmnopqrstuvwxyzABCDEFGHIJKLMNOPQRSTUVWXYZ"
+
+
+def program():
+    if "p" not in CACHE:
+        ops = build(CFG)
+        seq = [DIGITS.index(ORDER[i]) * 62 + DIGITS.index(ORDER[i + 1]) for i in range(0, len(ORDER), 2)]
+        sc = {"eng": QUEUE, "order": {e: [k for k in seq if QUEUE[k] == e] for e in "vapgsx"}}
+        CACHE["p"] = (ops, sc) + plan(ops, sc)
+    return CACHE["p"]
+
+
+def masks(core, peers, topo):
+    lists = [topo.engines(core, p) for p in peers]
+    few = min(len(x) for x in lists)
+    narrow = [i for i, x in enumerate(lists) if len(x) == few]
+    out, used = {}, set()
+    for grp in (narrow, [i for i in range(len(peers)) if i not in narrow]):
+        for a, i in enumerate(grp):
+            av = [e for e in lists[i] if e not in used]
+            k = len(av) // (len(grp) - a)
+            while k & (k - 1):
+                k -= 1
+            out[i] = av[:k]
+            used |= set(av[:k])
+    return [sum(1 << e for e in out[i]) for i in range(len(peers))], [len(out[i]) for i in range(len(peers))]
+
+
+def rank_program(g, core, T, topo):
+    rank = T.rank_of(core)
+    if rank is None:
+        return
+    ops, sc, keep, count = program()
+    N = len(T.cores)
+    queue = {"v": g.vector, "a": g.scalar, "p": g.tensor, "g": g, "s": g.sync}
+
+    def peers(r, sign):
+        return [T.cores[(r + sign * d) % N] for d in range(1, N)]
+    arrive = {}
+    for o in ops:
+        if o.get("send"):
+            k, sign = o["impl"]["g"][2][0], o["impl"]["g"][2][4]
+            froms = [(rank - sign * d) % N for d in range(1, N)]
+            arrive["ar%d" % k] = sum(masks(T.cores[r], peers(r, sign), topo)[1][d] for d, r in enumerate(froms))
+    sent = 0
+    for e in "sagvp":
+        q = queue[e]
+        for k, waits in keep[e]:
+            for j in waits:
+                s, c = count[j]
+                q.wait_ge(T.sem[s], arrive.get(s, c))
+            f = ops[k]["impl"][e][2]
+            if ops[k].get("send"):
+                x, src, dst, off, sign = f
+                ps = peers(rank, sign)
+                mk, ne = masks(core, ps, topo)
+                trs = []
+                for d, p in enumerate(ps):
+                    rid, pid = topo.addr(p, core)
+                    trs.append(RemoteDMATransfer(dst_ids=[DstId(rid=rid, pnc=pid)], dma_engine_mask=mk[d], remote_sem=T.sem["ar%d" % x],
+                                                 src=T[src][:, NB * d:NB * d + NB], dst=T[dst][:, off + NB * d:off + NB * d + NB]))
+                q.remote_dma_fused(trs, local_sem=T.sem.loc)
+                sent += sum(ne)
+                continue
+            ins = f(q, T)
+            if k in count:
+                ins.then_inc(T.sem[count[k][0]], 16 if ops[k].get("sem") else 1)
+        if e == "g":
+            q.wait_ge(T.sem.loc, sent)
+        if e == "s":
+            for o in ops:
+                if o.get("final"):
+                    q.wait_ge(T.sem[o["sem"]], 16)

@@ -5,38 +5,67 @@ ALU = AluOpType
 FN = ActivationFunctionType
 V, W, GH, NB, LW = 1536, 1920, 384, 128, 120
 MAGIC = 12582912.0
+EPS = 2.0 ** -14
 OWN = [(0, 512), (512, 1024), (1024, V)]
+T4 = [(0, 512), (512, 1024), (1024, 1408), (1408, V)]
 CFG = {
-    "na": 1760, "piece": 608,
-    "xp": [(V, W), (0, 1024), (1024, V)], "xc": [(V, W)] + OWN, "kp": OWN, "ec": OWN + [(V, W)], "lp": [(0, 960), (960, W)],
-    "s1": [(V, W, "mix"), (0, 512, "pe"), (512, 1024, "mix"), (1024, V, "mix")],
-    "s2": [(V, W, "pe"), (0, 512, "pe"), (512, 1024, "mix"), (1024, V, "mix")],
-    "u2": [(0, 512, "dbl"), (512, 1024, "mix"), (1024, 1280, "mix"), (1280, V, "mix")],
-    "u1": [(0, 512, "dbl"), (512, 1024, "mix"), (1024, 1280, "mix"), (1280, V, "mix")],
-    "flip": (0, 2),
-    "banks": {"D": [6, 7], "y": [5, 6, 7], "e": [0, 1, 2], "u": [3, 4], "kp": [0, 6], "za": [1, 7], "m": [2], "f": [5], "sm": [0, 1],
-              "kl": [2, 0, 1], "xh": [3, 4, 2, 0], "um": [0, 1, 2]},
+    "na": 2016, "piece": 320,
+    "xp": OWN + [(V, W)], "xc": T4[:2] + [(V, W)] + T4[2:], "lp": [(0, 960), (960, W)],
+    "s1": [(0, 768), (768, V)],
+    "s2": [(V, W, "T"), (0, 512, "T"), (512, 1024, "C"), (1024, V, "C")],
+    "u2": "DDCC", "u1": "DCCC",
+    "s1d": "D", "kd": True,
+    "yv": (0, 512, 1024, 1408),
 }
-QUEUE = "asssvvaagaavggvvaavvvggvvvvvvvvvvggggggggvagggggggggggggggggggggggggggvavvvvvgxvapvaaavvvvssppavppavaavpvvvvvvvaaavaaavapppvappvpppvappapppvappapppvappvpvpapvpapapapapapapapapaavvvavvvavvvapvppappvapvppappvapvppappvppppvpavpvvvvvppvvvvsvvsaavvvgxaaaappppaavvvavvvpvpvpvvvvvvvvgxaapvvaapvaaapavaapavvppvvppvvppvvppvvaavvvvavvaapppvavppvpppvavppapppvavppvpppvavppvpaapaapaapavpavpavpaapaapaapavpavpavvvvvavvvavvvapvppappvapvppappvapvppappvppppvpavpvvvvvpvvvsaaaaappppagxaaaappppvvvvvvvvvpvpvpvvvvvvvagxvpvaavaspaaavvppaavvvppavvvvppaavvvppaaavvppasavvvppasavvvppasvvvvppas"
-ORDER = "0002050l01030w0r06070u0t0s040n0q080o0p0v0a0d0j0b0g1d0h0c0f0k091c1h1i0O0i1j0e0x1k0m1m1o1e0J1p1f1n1q0y1g0z1u0M1r0A1l1t0S1v1y1w1z1s1A1x0K1O1L0L1P1K0T24291B1N0N1E1D1W1M1C0B2h1R0V1F1G1Q0Q2c1U1T1X2u0U1S251Y0W2d2v1Z262717202k0C1V1H2e0R2s2f282l0D2t2m2g0P212n2a223e232o0E2i1I102p2b2q180F2w2j2r1135192x2Q2y1J2A0Y0G2R332B2U142S2E3c2z2V0X2F2C2T0Z3t2D2W2Y152G342I2H2Z12362J3l2X37162K3230382L133d393b2O313k2M0H3a3f0I3n3g3m3h2N1a3y2P1b3i3z3o3j3B3p3q3C3D3r3E3u3s3F3S3G3v473T3w3Y48403H3x3I4f3A4b3J4j3K3U423Z3L3M3N3O41433P443V3Q454c3W463X493R4h4a4u4d4e4v4l4m4K4w4n4o4p4E4q4r4P4O4J4s4T4g4t4S4X4z4W4x4i4Q4y4Y4A4R4U4Z51504F4V524B5354554G4k4C584D4H4L5b844I5m595y4M5p5e575E4N5z5d5g5q5a565A5c5h5i5f5r5v5j5B5k5H5s5C5I5J5l5t5K5n5Q5o5L5D5N6U5u5F5M5w5G5O5x5T5P6L6M6q6u6O6r5U6F5R5Z6s6D606v6y5W6t6C656E666w5X6V5Y6x6G6b6H6z6I6c6N6J5S6X6A6P626Q6K636B6R5V6S6d6W686T6Y6Z6770616964716h727b7q7L737n7H7o7r7M7p7s7y7N7t7u7I7v7C7z7w7T7J7x7A7D6e7O7B7E7P7K6i7F747G6f6a7V6k7W6g6n7X7Y786o7Z6l807R797c75817d7e7U827f837g7h7Q7m7S6m8p6j6p768s8z8e8A8c8B8f8g8l8C8i8h8d8m8j8n8w8k8t8o8D8E8u8q8F8v778x7a8r7i908y7j857k8G8S947l868O8I8H958K8P8W878J8Q8L888R8X8T8a8Y968Z978M91898U8N9899928V939a8b9b"
+ORDER = """
+pc zb zc ld_nxt z2row ones i1 zpki i16k/a znomay on pd im120/a z1row crow.3 ih/v im257/v lvs imh/a br/v ld_x ld_shw i4k/a shu/a pf/a oe idi border.0
+ld_th qc/a iv0 prawm praw/a sca.0 scv.0 iv1 sca.1 idf s0/v scv.1 zlw.0 crow.1 send0 di.1 di.0 nw gt border.1 in13/v di.2 di.3 ie27/a pr16/a thn zpk
+dei.0 x161.3 ie15/a dei.1 nd1n/a q1n/a arrive0 cc border.2 dei.2 dei.3 xo1.7/a imq/g x161.0 xo1.4/a crow.0 c1 bp0 c2 x161.2 blq xo1.1/v pi nd1p/a
+xo1.0/v yb1.0 xd1.2 bt xo1.5/a xd1.0 yb1.1 ya1.1 xo1.3/a yb1.2 nb.1 xd1.1 bf ya1.0 anti xo1.6/a xo1.2/a xd1.3 xi1.0/a xi1.1/a rd1.3/a xd1.4 yc1.0 d1.0
+x161.1 bl/a yb1.4 xd1.5 ps1n/a gs yb1.3 x161.4 ad1.0 nb.0 yc1.1 d1.1 fm1/a ya1.2 yc1.2 ad1.2 xd1.7 ya1.3 xd1.6 ad1.1 q1p/a bfn/a yc1.3 d1.2 ad1.3 e1.0
+key1.0/v nb.2 kwz e1.2 ya1.4 yc1.4 nb.3 d1.3 key1.2/a ad1.4 nka1 e1.1 key1.1/v nkb1/a e1.3 nb.4 im16k/g key1.3/a e1.4 key1.4/v th0 rd1.4/v k1.0/a
+im1/g crow.2 zlw.5 crow.4 thd u1.5 k1.1/a r1.5/v rd1.1/a iq/g u1.4 rd1.2/a r1.4/a kc1.0 bp1 kc1.1 u1.2 u1.3 r1.3/a kc1.3 kc1.2 rd1.0/a u1.1 r1.1/a
+u1.0 kc1.4 r1.0/a lv1.0 zlw.1 fs1.0 zlw.2 k1.2/a kc1.6 zlw.3 rd1.5/a r1.2/a ma1.0 id16/a s1.3/a ma1.1 ma1.2 kc1.5 s1.2/a m1.0 ma1.3 b1p/a kc1.7 lv1.1
+fs1.1 kl1.0/a k1.3/a fs1.2 m1.1 kc1.8 s1.1/a kc1.9 s1.0/a lv1.2 kl1.1/a kc1.10 kc1.11 lv1.3 n1.0 pk1.0 m1.2 n1.1 pk1.1 kl1.2/a m1.3 n1.2 pk1.2 zlw.6
+kl1.3/a n1.3 pk1.3 fs1.3 sw1.0 bfs/a f1/v sw1.1 cc1 sa1g/a lvq1 xb1.0 to1.0 xb1.1 sb1.1/a sc1g.0 sc1g.1 zlw.7 lvs1/v sc1g.2 to1.1 xa1.0 to1.2 to1.3
+xa1.2 zlw.4 o1.2 send1 arrive1 xa1.1 xa1.3 sb1.0/a ff1.0 lw1.0 ff1.1 ps1pm o1.1 sa1.0/a sd1.1 xn2.2 ps1p/a o1.0 sd1.0 xn2.1 sa1.1/a sc1.1 sc1.0 outa1
+home1.0 homes1.0 o1.3 h1.3 xn2.0 home1.1 homes1.1 home1.2 homes1.2 lw1.1 outb1 lk.0/a lk.1/a lq.0 xm2.1 h1.0 send2 arrive2 h1.2 nd2.0/v lk.3/a lk.2/a
+lq.1 xm2.0 h1.1 lk.7/v xm2.2 xe2.0/v nd2.1/v lk.4/a lk.5/a lq.2 xe2.1/a r16.1 r16.0 xg2/v x162.3 x162.1 lk.6/a lq.3 xe2.2/a xo2.1/v nd2.3/v x162.0
+nd2.2/a xd2.2 q2.2/a nka2 q2.1/a xo2.0/v xo2.5/a xd2.3 xd2.0 yb2.1 xo2.2/a xo2.6/a ya2.1 xo2.4/a xd2.1 yb2.3 yb2.0 yc2.1 d2.1 xd2.4 ya2.0 xo2.3/a
+xo2.7/a yb2.2 rs2.0 yc2.0 d2.0 xi2.1/a x162.2 xi2.0/a u2.3 ya2.2 yc2.2 xd2.5 ya2.3 r2.3 xd2.6 xd2.7 ad2.0 adc.0 yc2.3 d2.2 ad2.1 adc.1 rm2.0 yb2.4
+ya2.4 yc2.4 ad2.2 d2.3 ad2.3 adc.3 e2.0 key2.0/a e2.1 e2.3 adc.2 e2.2 key2.1/v nkb2/a ad2.4 adc.4 e2.4 r16.2 key2.4/v q2.3/v ma2.1 key2.3/a key2.2/a
+k2.0/v q2.0/a k2.3/a kd2.6 kb2.0/a k2.2/a kd2.0 k2.1/a u2.4 r2.4 kd2.4 lv2.0 rs2.1 kd2.1 u2.0 kd2.2 lb2.0 rs2.2 r2.0 u2.2 lv2.1 kb2.1/a kd2.3 ma2.2
+ma2.0 lv2.2 m2.0 r2.2 lb2.1 ma2.3 kb2.2/a kd2.5 b2/a lv2.3 kb2.3/a kd2.7 ra2.0 m2.1 rs2.4 lb2.2 m2.2 h2.0 h2.1 ul1/a lb2.3 m2.3 h2.2 ua.0 pk2.0/a
+pk2.1/a pk2.2/a h2.3 pk2.3/v sp2g.3/v sp2g.0/v ua.2 fq/a ps2m sp2g.1/a to2.2 sp2g.2/a sa2.1/a sa2.0/v sc2.0 ua.3 sm2g se2g/a to2.0 ub.0 to2.1 to2.3
+sp2.2/a sp2.0/a sp2.1/a sp2.3/a ps2/a sc2.3 sc2.1 sc2.4 send3 arrive3 ub.2 u2.5 sm2 se2/a fm16k/a sc2.2 sc2.5 home2.0 homes2.0 home2.1 homes2.1 ub.3
+r2.5 u2.1 ua.1 lvq2 lvr2 home2.2 rs2.5 homes2.2 rm2.1 lvt2/v xa2.0 xa2.1 ra2.2 rm2.2 xa2.2 ub.1 r2.1 ra2.5 out2/a send4 sw2 rs2.3 xa2.3 rm2.5 rm2.3
+ra2.1 ra2.4 ra2.3 fs2.0 rm2.4 ff2.0 fs2.1 ff2.1 fs2.2 ul2/v arrive4 ug2.0/a fs2.3 wa ug2.1/a cc2 lc2 xb2 ug2.5/v uc2.7 wg ug2.2/a fa2 uc2.0 um2.0
+ug2.4/a uc2.1 um2.1 ug2.3/a w1.0/a uc2.2 um2.2 uc2.4 uc2.3 um2.3 uc2.5 uc2.6 uc2.8 uc2.9 um2.4 w1g/v fb2 lw2 w1.1/a um2.5 w1.3/v w1.2/a ug1.1/v
+ug1.0/a uc1.0 uc1.1 um1.0 ug1.3/a um1.1 ug1.2/a uc1.2 ug1.4/a uc1.8 uc1.3 uc1.5 yn.0/a uc1.4 um1.2 yn.2/a uc1.6 uc1.9 uc1.7 um1.3 y.0 st_x.0 y.1
+st_x.1 uc1.10 y.2 yn.1/a um1.4 st_x.2 yn.3/a st_yn y.3 st_x.3
+"""
 I32, U16, F32, F16, B16 = "int32", "uint16", "float32", "float16", "bfloat16"
 SB = {}
-for _d, _l in ((I32, "nxi:240 shi:24 thi:4 xi:1920 d32:1920 s32:1536 s0:384 pi:240 pc:4 pd:4"),
-               (U16, "shu:24 praw:240 nd1:480 nd2:480 ps1:480 ps2:240 ul1:480 ul2:480"),
-               (F32, "thb:4 xw2:1920 kw:1920 t:1536 pk:1920 hh:1920 hg1:384 hg2:384 rc1:384 rc2:384 tm:384 s1:384 s2:384 w2:1920 "
-                     "z1:3840 z2:3840 lw:3840 iv:1792 zc:240 c1:240 c2:240 idf:480 pf:4 lvs:120 cc:120 lc:120 t1:480 ff:480 f1:128 fq:128 f2k:128"),
-               (F16, "ab:7680 gg:7680 ad:1920 adc:1920 lv1:1536 lv2:1536 sg:1536 rr:6144 h1:1536 h2:1536 r16:1920 qc:240 br:240 b16:480 "
-                     "pr16:240 q1:480 q2:480 id16:480 im257:128 ibeta:128 im2047:128"),
-               (B16, "nomay:1536 nb:1920 big:128 ones:512 zb:128 crow:384 nw:128 gs:128 gt:144 bt:144 bf:144 bfn:144 bfs:144 bp0:144 bp1:144 "
-                     "di:512 i1:128 im1:128 imq:128 imh:128 i4k:128 im120:128 ieps:128")):
+for _d, _l in ((I32, "nxi:240 shi:24 thi:4 xi:1920 xw2:1920 pki:1920 s0:384 pi:240 pc:4 pd:4"),
+               (U16, "shu:24 nk:96 praw:240 nd1:480 nd2:480 ps1:480 ps2:240 ul1:480 ul2:480"),
+               (F32, "thn:4 kw:1928 bl:96 nkf:96 t:1536 pk:1920 hh:1920 hg1:384 rc1:384 tm:384 s1:384 s2:384 w2:1920 z1:3840 z2:3840 "
+                     "lw:3840 iv:2112 zc:240 c1:240 c2:240 idf:480 pf:4 lvs:120 cc:120 xb:240 ff:480 f1:128 fm1:128 fq:128 fm16k:128"),
+               (F16, "ab:7680 gg:4096 nb:1920 d16:1536 ad:1920 adc:1920 lva:1536 lvb:1536 hg2:384 rc2:384 rr:7680 h1:1536 h2:1536 "
+                     "r16:1536 x16:1920 qc:240 br:240 b16:480 pr16:240 q1:480 q2:480 id16:480 im257:128 thd:128 th0:128"),
+               (B16, "nomay:1536 ones:512 oe:512 on:512 zb:128 crow:640 nw:128 gs:128 gt:144 bt:144 bf:144 bfn:144 bfs:144 "
+                     "bp0:144 bp1:144 di:512 anti:128 i1:128 im1:128 imq:128 imh:128 iq:128 ih:128 i4k:128 i16k:128 im16k:128 im120:128 "
+                     "ie27:128 ie15:128 in13:128")):
     for _x in _l.split():
         SB[_x.split(":")[0]] = (int(_x.split(":")[1]), _d)
-SCALED = {"im1": -1.0, "imq": -0.25, "imh": -0.5, "i4k": 4096.0, "im120": -120.0, "ieps": 1.0 / 2048, "im257": -257.0,
-          "ibeta": 2047.0 / 4096, "im2047": -2047.0, "f1": 1.0, "fq": 0.25, "f2k": 2048.0}
+SCALED = {"im1": -1.0, "imq": -0.25, "imh": -0.5, "iq": 0.25, "ih": 0.5, "i4k": 4096.0, "i16k": 1 / EPS, "im16k": -1 / EPS,
+          "im120": -120.0, "im257": -257.0, "ie27": EPS / 16384, "ie15": EPS / 2, "in13": -1.0 / 16384,
+          "f1": 1.0, "fm1": -1.0, "fq": 0.25, "fm16k": -1 / EPS}
+IDENT = {1.0: "i1", -1.0: "im1", -0.25: "imq", -0.5: "imh", 0.25: "iq", 0.5: "ih"}
 SCRATCH = {k: ("sbuf", [128, n], d) for k, (n, d) in SB.items()}
 for _k in range(8):
     SCRATCH["bank%d" % _k] = ("psum", [128, 512], F32)
-SEMAPHORES = ["ev", "ea", "ep", "eg", "loc"] + ["ar%d" % k for k in range(5)] + ["dm%d" % k for k in range(16)]
+SEMAPHORES = ["ev", "ea", "ep", "eg", "loc"] + ["ar%d" % k for k in range(5)] + ["dm%d" % k for k in range(20)]
+BANK = {}
 
 
 def S(buf, lo, hi, step=1, p=None):
@@ -58,13 +87,13 @@ def two(r):
 def ap(T, r):
     if isinstance(r, (int, float)):
         return r
-    t = T["bank" + r[0][1:]] if psum(r) else T[r[0]]
+    t = T["bank%d" % BANK[r[0]]] if psum(r) else T[r[0]]
     p = slice(0, 128) if r[4] is None else slice(r[4][0], r[4][1], r[4][2])
     return t[p, r[1]:r[2]] if r[3] == 1 else t[p, r[1]:r[2]:r[3]]
 
 
 def build(C):
-    ops, acc, ntile, ndma = [], {}, {}, [0]
+    ops, acc, ntile, ndma = [], {}, [0], [0]
 
     def meet(a, b):
         if a[1] >= b[2] or b[1] >= a[2]:
@@ -72,19 +101,20 @@ def build(C):
         return a[4] is None or b[4] is None or len(set(range(*a[4])) & set(range(*b[4]))) > 0
 
     def add(name, impl, reads, writes, **kw):
-        k, deps = len(ops), set()
+        k, deps, tiles = len(ops), set(), set()
         for r, wr in [(r, False) for r in reads if isinstance(r, tuple)] + [(r, True) for r in writes]:
-            for (j, q, wq) in acc.get(r[0], [])[-12 if psum(r) else 0:]:
+            for (j, q, wq) in acc.get(r[0], [])[-2 if psum(r) else 0:]:
                 if j != k and (psum(r) or ((wr or wq) and meet(r, q))):
                     deps.add(j)
             acc.setdefault(r[0], []).append((k, r, wr))
-        ops.append(dict(kw, name=name, impl=impl, deps=deps))
+            if psum(r):
+                tiles.add(r[0])
+        ops.append(dict(kw, name=name, impl=impl, deps=deps, tiles=tiles))
         return k
 
-    def tile(pool, m):
-        banks = C["banks"][pool]
-        ntile[pool] = ntile.get(pool, -1) + 1
-        return S("#%d" % banks[ntile[pool] % len(banks)], 0, m)
+    def tile(m):
+        ntile[0] += 1
+        return S("#%d" % ntile[0], 0, m)
 
     def vts(o, i, s1, s2, op0, op1=None):
         n = width(i) * (0.5 if two(o) and two(i) else 1)
@@ -93,16 +123,25 @@ def build(C):
         return ("v", n, lambda q, T: q.tensor_scalar(ap(T, o), ap(T, i), s1, s2, op0, op1))
 
     def aact(o, i, f, bias, scale):
-        return ("a", width(i), lambda q, T: q.activation(ap(T, o), ap(T, i), f, bias=ap(T, bias), scale=scale))
+        return ("a", width(i), lambda q, T: q.activation(ap(T, o), ap(T, i), f, bias=bias, scale=scale))
+
+    def gsel(o, i, pat, op, fl, base, cm):
+        return ("g", width(o), lambda q, T: q.affine_select(ap(T, o), ap(T, i), pat, op, fl, base, cm))
 
     def ts(name, o, i, s1, s2, op0, op1=None):
         add(name, {"v": vts(o, i, s1, s2, op0, op1)}, [i, s1], [o])
 
     def act(name, o, i, f, bias=0.0, scale=1.0):
-        add(name, {"a": aact(o, i, f, bias, scale)}, [i, bias], [o])
+        add(name, {"a": aact(o, i, f, bias, scale)}, [i], [o])
 
     def lin(name, o, i, scale, bias):
         add(name, {"v": vts(o, i, scale, bias, ALU.mult, ALU.add), "a": aact(o, i, FN.Identity, bias, scale)}, [i], [o])
+
+    def relu(name, o, i, c):
+        add(name, {"v": vts(o, i, c, c, ALU.max, ALU.subtract), "a": aact(o, i, FN.Relu, -c, 1.0)}, [i], [o])
+
+    def copy(name, o, i):
+        add(name, {"g": gsel(o, i, [[0, width(o)]], ALU.is_ge, 0.0, 0, 0)}, [i], [o])
 
     def tt(name, o, a, b, op):
         n = width(a) * (1 if psum(a) or psum(b) else 2)
@@ -133,7 +172,7 @@ def build(C):
             for k, (l, r) in enumerate(terms):
                 ins = q.matmul(ap(T, o), ap(T, l), ap(T, r), start and k == 0, stop and k == len(terms) - 1)
             return ins
-        add(name, {"p": ("p", (cyc, len(terms)), f)}, [x for lr in terms for x in lr], [o])
+        add(name, {"p": ("p", cyc, f)}, [x for lr in terms for x in lr], [o])
 
     def I(name):
         return S(name, 0, 128)
@@ -147,9 +186,6 @@ def build(C):
     def iota(name, o, pat, base, cm):
         kw = {} if SB[o[0]][1] == I32 else {"allow_small_or_imprecise_dtypes": True}
         add(name, {"g": ("g", width(o), lambda q, T: q.iota(ap(T, o), pat, base, cm, **kw))}, [], [o])
-
-    def gsel(o, i, pat, op, fl, base, cm):
-        return ("g", width(o), lambda q, T: q.affine_select(ap(T, o), ap(T, i), pat, op, fl, base, cm))
 
     def sel(name, n, src, pat, op, base, cm, lo=0):
         o, i = S(name, lo, lo + n), S(src, 0, n)
@@ -181,7 +217,7 @@ def build(C):
     POSC = 120.0 * 1920 + 3839.0 * 1030
 
     def positions(name, o, q, b):
-        tl = tile("D", 240)
+        tl = tile(240)
         mm(name + "m", tl, [(I("im120"), q), (I("i4k"), b), (I("im257"), b)])
         lin(name, o, tl, -1.0, POSC)
         return tl
@@ -203,33 +239,33 @@ def build(C):
         add(k, impl, [I("i1"), I("zb")], [I(k)])
     NA, PC = C["na"], C["piece"]
     iota("iv0", S("iv", 0, PC), [[1, PC]], 64, 0)
-    iota("iv1", S("iv", PC, NA), [[1, NA - PC]], 64 + PC, 0)
+    iota("iv1", S("iv", PC, max(NA, W)), [[1, max(NA, W) - PC]], 64 + PC, 0)
     fill("ones", S("ones", 0, 512), 1.0)
-    for k, c in enumerate([MAGIC, -MAGIC, 0.375]):
+    fill("oe", S("oe", 0, 512), EPS / 16384)
+    fill("on", S("on", 0, 512), -1.0 / 16384)
+    for k, c in enumerate([MAGIC, -MAGIC, 0.375, MAGIC * EPS, -MAGIC * EPS]):
         fill("crow", cst(k, 1)[0], c)
-    NW = S("nw", 0, 128, 1, (0, 64, 1))
-    fill("nw", NW, 0.0)
-    fill("nw", S("nw", 0, 128, 1, (0, 1, 1)), 1.0 / 2048)
-    fill("nw", S("nw", 0, 128, 1, (32, 33, 1)), 1.0 / 32)
-    fill("big", I("big"), 4096.0)
+    NW = S("nw", 0, 128, 1, (0, 1, 1))
+    fill("nw", NW, 1.0 / 2048)
     fill("lvs", S("lvs", 96, LW), 0.0)
-    fill("lc", S("lc", 96, LW), 0.0)
+    fill("cc", S("cc", 96, LW), 0.0)
     for k in range(4):
         sel("di", 128, "ones", [[16, 8], [1000, 2], [2, 8]], ALU.is_equal, k // 2 - 1000 * (k % 2), -1, 128 * k)
     sel("gt", 128, "ones", [[-16, 8], [0, 16]], ALU.is_ge, 0, 1)
     sel("gs", 128, "gt", [[16, 8], [0, 16]], ALU.is_ge, 15, -1)
     sel("bt", 144, "ones", [[16, 9], [1000, 16]], ALU.is_ge, 15 - 15000, -1)
     sel("bf", 144, "bt", [[-16, 9], [0, 16]], ALU.is_ge, 0, 1)
-    lin("bfn", S("bfn", 0, 144), S("bf", 0, 144), -1.0, 0.0)
-    lin("bfs", S("bfs", 0, 144), S("bf", 0, 144), 1.0 / 16, 0.0)
+    for name, c in (("bfn", -1.0), ("bfs", 1.0 / 16)):
+        lin(name, S(name, 0, 144), S("bf", 0, 144), c, 0.0)
     for r in range(2):
         sel("bp%d" % r, 144, "ones", [[16, 9], [1000, 16]], ALU.is_equal, r - 15000, -1)
-    for lo in range(0, W, 384):
-        iota("nb0", S("nb", lo, lo + 384, 1, (0, 32, 1)), [[0, 6], [1, 64]], 0, 0)
-        iota("nb1", S("nb", lo, lo + 384, 1, (32, 64, 1)), [[1, 6], [0, 64]], lo // 64, 0)
-    for buf, a, b, n in (("nomay", 0, V, 384), ("pk", V, W, 384), ("lw", 0, 2 * W, 480)):
-        for lo in range(a, b, n):
-            iota("z" + buf, S(buf, lo, lo + n), [[0, n]], 0, 0)
+    for lo, hi in C["xc"]:
+        copy("nb", S("nb", lo, hi, 1, (0, 32, 1)), S("iv", lo, hi, 1, (0, 32, 1)))
+    fill("znomay", S("nomay", 0, V), 0.0)
+    fill("zpk", S("pk", V, W), 0.0)
+    fill("zpki", S("pki", V, W), 0)
+    for lo in range(0, 2 * W, 480):
+        iota("zlw", S("lw", lo, lo + 480), [[0, 480]], 0, 0)
     ID = S("idf", 0, 480)
     iota("idi", ID, [[0, 2], [1, 2], [32, LW]], 0, 0)
     iota("pc", S("pc", 0, 1), [[0, 1]], 0, 2)
@@ -237,7 +273,10 @@ def build(C):
     lin("pf", S("pf", 0, 1), S("pd", 0, 1), 1.0, 0.0)
     ts("idf", ID, ID, S("pf", 0, 1), None, ALU.add)
     lin("id16", S("id16", 0, 480), ID, 1.0, -1920.0)
-    lin("thb", S("thb", 0, 1), S("thi", 0, 1), -1.0, -4095.5)
+    ts("thn", S("thn", 0, 1), S("thi", 0, 1), 2047.0, -1.0, ALU.min, ALU.mult)
+    ts("th0", I("th0"), I("i1"), S("thn", 0, 1), None, ALU.mult)
+    add("anti", {"g": gsel(I("anti"), I("zb"), [[1, 128]], ALU.not_equal, 0.5, -127, 1)}, [I("zb")], [I("anti")])
+    tt("thd", I("thd"), I("th0"), I("anti"), ALU.add)
 
     lin("shu", SH, S("shi", 0, 24), 1.0, 0.0)
     gat("s0", S("s0", 0, GH), S("xi", 0, V), SH)
@@ -258,12 +297,12 @@ def build(C):
             add("scv", {"v": ("vs", hi - lo, lambda q, T: q.tensor_scalar(ind(T, z, idx), ap(T, i), 1.0, float(lo), ALU.mult, ALU.add))}, [idx, i], [z])
     scatter("a", 0, PC)
     scatter("a", PC, NA)
-    for lo in range(NA, 2 * W, PC):
-        scatter("v", lo, min(lo + PC, 2 * W))
+    scatter("v", NA, NA + PC)
+    scatter("v", NA + PC, 2 * W)
     dma("c1", S("c1", 0, 240), row("z1"), RB)
     dma("c2", S("c2", 0, 240), row("z2"), RB)
     for src in ("qc", "pr16"):
-        tl = tile("D", 240)
+        tl = tile(240)
         for j in range(2):
             mm("dei", lst(tl[0], j), [(S("di", 128 * (2 * j + h), 128 * (2 * j + h) + 128), S(src, h, 240, 2)) for h in range(2)])
         if src == "qc":
@@ -278,140 +317,192 @@ def build(C):
     lin("b1p", S("b16", 0, 240), PI, 1.0 / 32, 1028 - 31.0 / 64)
     positions("ps1p", S("ps1", 0, 240), S("q1", 0, 240), S("b16", 0, 240))
     for d in range(3):
-        sca("border", S("nomay", 0, V), S("shu", 8 * d, 8 * d + 8), I("big"))
+        sca("border", S("nomay", 0, V), S("shu", 8 * d, 8 * d + 8), S("ones", 0, NB))
+    tl = tile(96)
+    squeeze("blq", tl, "bp0", "nomay", 0, V)
+    lin("bl", S("bl", 0, 96), tl, 3840.0, -1920.0)
+    fill("kwz", S("kw", W, W + 8), -1.0)
+
+    def nbr(j, lo, hi):
+        return S("ab", W * j + lo, W * j + hi)
+
+    def combo(lo, hi, co):
+        co = list(co)
+        for j in (0, 1):
+            if lo < V:
+                co[2 + j] += co[j]
+        return [(I(IDENT[co[j]]), nbr(j, lo, hi)) for j in range(4) if co[j]]
 
     def level(lev):
         n = "%d" % lev
-        win, nd, qq, lv, size = ("xi" if lev == 1 else "xw2"), "nd" + n, "q" + n, "lv" + n, ("ad" if lev == 1 else "adc")
-
-        def nbr(j, lo, hi):
-            return S("ab", W * j + lo, W * j + hi)
-
-        def key(lo, hi):
-            return [(NW, S("nb", lo, hi, 1, (0, 64, 1))), (I("gs"), S(size, lo, hi))]
-        for j in (2, 3, 0, 1):
+        win, nd, qq, size = ("xi" if lev == 1 else "xw2"), "nd" + n, "q" + n, ("ad" if lev == 1 else "adc")
+        beta, keys = (0.75 if lev == 1 else 0.0), {}
+        for j in (2, 3):
             for lo, hi in C["xp"]:
-                gat("x" + n, nbr(j, lo, hi), S(win, 0, W), lst(nd, j, lo, hi), -0.375)
+                gat("xo" + n, nbr(j, lo, hi), S(win, 0, W), lst(nd, j, lo, hi), -beta)
         for lo, hi in C["xc"]:
-            tl, d = tile("y", hi - lo), S("d32", lo, hi)
-            mm("yb" + n, tl, [(I("imq"), nbr(j, lo, hi)) for j in (2, 3)], True, False)
-            mm("ya" + n, tl, [(I("imq"), nbr(0, lo, hi))], False, False)
-            mm("ya" + n, tl, [(I("imq"), nbr(1, lo, hi))], False, True)
-            tt("d" + n, d, tl, S(win, lo, hi), ALU.add)
-            act("ad" + n, S("ad", lo, hi), d, FN.Abs)
+            for j in (0, 1):
+                if lo < V:
+                    gop("xd" + n, nbr(j, lo, hi), S(win, 0, W), lst(nd, j, lo, hi), nbr(2 + j, lo, hi), ALU.subtract)
+                else:
+                    gat("xi" + n, nbr(j, lo, hi), S(win, 0, W), lst(nd, j, lo, hi))
+        for lo, hi in C["xc"]:
+            m, tl, d = hi - lo, tile(hi - lo), S("d16", lo, hi)
+            c = combo(lo, hi, [-0.25] * 4)
+            mm("yb" + n, tl, c[2:] + ([cst(2, m)] if lev == 2 else []), True, False)
+            mm("ya" + n, tl, c[:1], False, False)
+            mm("yc" + n, tl, c[1:2] + [(I("i1"), S("x16", lo, hi))] + ([] if lo < V else [cst(0, m), cst(1, m)]), False, True)
+            if lo < V:
+                ts("d" + n, d, tl, MAGIC, MAGIC, ALU.add, ALU.subtract)
+            act("ad" + n, S("ad", lo, hi), d if lo < V else tl, FN.Abs)
             if lev == 2:
                 ts("adc", S("adc", lo, hi), S("ad", lo, hi), 255.0, None, ALU.min)
-            tl = tile("e", hi - lo)
-            mm("e" + n, tl, key(lo, hi)[:1], True, False)
-            mm("eb" + n, tl, key(lo, hi)[1:], False, True)
-            lin("key" + n, S("kw", lo, hi), tl, 1.0, 0.0)
-        terms = [(0, 2, -1), (1, 3, -1), (0, 3, 1), (1, 2, 1)]
-        for k, (a, b, sgn) in enumerate(terms):
+            keys[lo] = tile(m)
+            mm("e" + n, keys[lo], [(NW, S("nb", lo, hi, 1, (0, 1, 1))), (I("gs"), S(size, lo, hi))])
+            lin("key" + n, S("kw", lo, hi), keys[lo], 1.0, 0.0)
+        tt("nka" + n, S("nkf", 0, 96), S(qq, 0, 96), S("bl", 0, 96), ALU.max)
+        lin("nkb" + n, S("nk", 0, 96), S("nkf", 0, 96), 0.5, 959.75)
+        slots = []
+        for a, b in ((0, 2), (1, 3), (0, 3), (1, 2)):
+            k, straight = len(slots), b == a + 2
+            slots.append("bf" if lev == 1 and not straight else "bfn")
             for lo, hi in OWN:
-                tl, r = tile("u", hi - lo), S("rr", V * k + lo, V * k + hi)
-                mm("u" + n, tl, [(I("im1"), nbr(b, lo, hi)), (I("i1"), nbr(a, lo, hi))])
+                r, u = S("rr", V * k + lo, V * k + hi), nbr(a, lo, hi)
+                if not straight:
+                    u = tile(hi - lo)
+                    mm("u" + n, u, combo(lo, hi, [1.0 if j == a else -1.0 if j == b else 0 for j in range(4)]))
                 if lev == 1:
-                    add("r1", {"v": vts(r, tl, 0.0, None, ALU.max), "a": aact(r, tl, FN.Relu, 0.0, 1.0)}, [tl], [r])
+                    relu("rd1" if straight else "r1", r, u, beta)
+                elif straight:
+                    act("rs2", r, u, FN.Abs)
+                    ts("rm2", r, r, 255.0, None, ALU.min)
                 else:
-                    act("r2", r, tl, FN.Abs)
-                    if k in C["flip"]:
-                        act("r2a", r, r, FN.Relu, 255.0, -1.0)
-                    else:
-                        ts("r2v", r, r, 255.0, None, ALU.min)
-        for lo, hi in C["kp"]:
-            t = S("t", lo, hi)
-            gat("k" + n, t, S("kw", 0, W), lst(nd, 0, lo, hi))
-            for j in (1, 2, 3):
-                gop("kc" + n, t, S("kw", 0, W), lst(nd, j, lo, hi), t, ALU.min)
-        for lo, hi in C["kp"]:
-            m, s, d, l, sg = hi - lo, S("s32", lo, hi), S("d32", lo, hi), S(lv, lo, hi), S("sg", lo, hi)
-            add("s" + n, {"v": vts(s, d, 2, None, ALU.arith_shift_right), "a": aact(s, d, FN.Identity, -0.375, 0.25)}, [d], [s])
-            tl = tile("kp", m)
-            mm("kp" + n, tl, key(lo, hi) + [(I("i1"), S("nomay", lo, hi))] + ([(I("i4k"), S("lv1", lo, hi))] if lev == 2 else []))
-            tt("lv" + n, l, tl, S("t", lo, hi), ALU.is_lt)
-            tl = tile("za", m)
-            mm("za" + n, tl, [(I("i1"), S("ad", lo, hi))], True, False)
-            mm("zb" + n, tl, [(I("i4k"), l)], False, True)
-            act("sg" + n, sg, tl, FN.Sign, S("thb", 0, 1))
-            tl = tile("m", m)
-            a, b = ("ieps", "ibeta") if lev == 1 else ("i1", "imh")
-            mm("m" + n, tl, [(I(b), S("ones", 0, m)), (I(a), l)], True, False)
-            mm("mb" + n, tl, [(I(b), sg)], False, True)
-            tt("pk" + n, S("pk", lo, hi), tl, s, ALU.mult)
-        tf = tile("f", 96)
-        for k, (a, b, sgn) in enumerate(terms):
-            if lev == 2 and k in C["flip"]:
-                sgn = -sgn
-            squeeze("f" + n, tf, "bf" if sgn > 0 else "bfn", "rr", V * k, V, k == 0, k == 3)
-        ts("cc" + n, S("cc", 0, 96), tf, 0.0, None, ALU.is_lt)
-        tl = tile("D", 96)
-        squeeze("lvq" + n, tl, "bfs", lv, 0, V)
-        lin("lvs" + n, S("lvs", 0, 96), tl, 1.0, 0.0)
-        tt("lc" + n, S("lc", 0, 96), S("lvs", 0, 96), S("cc", 0, 96), ALU.mult)
-        td, tx = tile("D", 480), tile("D", 480)
-        mm("d1" + n, td, [(I("i1"), S(qq, 0, 480)), (I("im1"), S("id16", 0, 480))])
-        for j in (2, 3, 0, 1):
-            tt("xa" + n, lst(tx[0], j), lst(td[0], j), S("lvs", 0, LW), ALU.mult)
-        tt("t1" + n, S("t1", 0, 480), tx, ID, ALU.add)
-        td, tx = tile("D", 240), tile("D", 240)
-        sides = (1, 0) if lev == 1 else (1,)
-        for k in sides:
-            mm("d2" + n, lst(td[0], k), [(I("i1"), lst(qq, 2 * k + 1)), (I("im1"), lst(qq, 2 * k))])
-        for k in sides:
-            tt("xb" + n, lst(tx[0], k), lst(td[0], k), S("lc", 0, LW), ALU.mult)
-        for k in sides:
-            tt("f0" + n, lst("ff", 2 * k), lst("t1", 2 * k), lst(tx[0], k), ALU.add)
-            tt("f1" + n, lst("ff", 2 * k + 1), lst("t1", 2 * k + 1), lst(tx[0], k), ALU.subtract)
-            dma("lw" + n, row("lw", 1 - k), S("ff", 240 * k, 240 * k + 240), RB)
-        lin("ul" + n, S("ul" + n, 0, 480), S("t1", 0, 480), 0.5, -0.25)
-        own, hg, PK = ("hh" if lev == 1 else "w2"), "hg" + n, S("pk", 0, W)
-        for lo, hi, mode in C["s" + n]:
-            o = S(hg, lo - V, hi - V) if lo >= V else S(own, lo, hi)
-            plain = lev == 1 or lo >= V
-            if mode == "mix":
-                if plain:
-                    gat("sa" + n, o, PK, lst(nd, 0, lo, hi))
-                else:
-                    gop("sa" + n, o, PK, lst(nd, 0, lo, hi), S("xw2", lo, hi), ALU.add)
+                    act("r2", r, u, FN.Abs)
+                    act("ra2", r, r, FN.Relu, 255.0, -1.0)
+        for lo, hi in T4:
+            t, t2, KW = S("t", lo, hi), S("w2", lo, hi), S("kw", 0, W)
+            gat("k" + n, t, S("kw", 0, W + 8), lst("nk", 0, lo, hi))
+            if lev == 1 or not C["kd"]:
                 for j in (1, 2, 3):
-                    gop("sc" + n, o, PK, lst(nd, j, lo, hi), o, ALU.add)
+                    gop("kc" + n, t, KW, lst(nd, j, lo, hi), t, ALU.min)
             else:
-                tl = tile("sm", hi - lo)
+                gat("kb2", t2, KW, lst(nd, 1, lo, hi))
+                gop("kd2", t, KW, lst(nd, 2, lo, hi), t, ALU.min)
+                gop("kd2", t2, KW, lst(nd, 3, lo, hi), t2, ALU.min)
+        for lo, hi in T4:
+            m, d, l, h = hi - lo, S("d16", lo, hi), S("lva", lo, hi), S("h" + n, lo, hi)
+            tt("lv" + n, l, keys[lo], S("t", lo, hi), ALU.is_lt)
+            tl = tile(m)
+            if lev == 1:
+                s = S("pki", lo, hi)
+                lin("s1", s, d, 0.25, -0.375)
+                far, kept = [(I("thd"), S("oe", 0, m)), (I("ie27"), S("ad", lo, hi))], [(I("ie15"), l), cst(3, m), cst(4, m)]
+                kl = S("lvb", lo, hi)
+                mm("ma1", tl, far, True, False)
+                mm("m1", tl, kept, False, True)
+                lin("kl1", kl, tl, 1.0, 0.0)
+                tl = tile(m)
+                mm("n1", tl, [(I("i1"), l), (I("i1"), kl)])
+                tt("pk1", S("pk", lo, hi), tl, s, ALU.mult)
+                tl = tile(m)
+                mm("o1", tl, [(I("i1"), kl)])
+                tt("h1", h, tl, d, ALU.mult)
+            else:
+                l2 = S("lvb", lo, hi)
+                if C["kd"]:
+                    tt("lb2", l2, keys[lo], S("w2", lo, hi), ALU.is_lt)
+                mm("ma2", tl, [(I("thd"), S("on", 0, m)), (I("in13"), S("ad", lo, hi))], True, False)
+                mm("m2", tl, ([(I("iq"), l), (I("iq"), l2)] if C["kd"] else [(I("ih"), l)]) + [cst(0, m), cst(1, m)], False, True)
+                tt("h2", h, tl, d, ALU.mult)
+                lin("pk2", S("pki", lo, hi), h, 0.25, -0.375)
+        tf = tile(96)
+        for k, mask in enumerate(slots):
+            squeeze("fs" + n, tf, mask, "rr", V * k, V, k == 0, k == len(slots) - 1)
+        ts("cc" + n, S("cc", 0, 96), tf, 0.0 if lev == 1 else -2 * 16 * 255.0, None, ALU.is_lt)
+        tl = tile(96)
+        squeeze("lvq" + n, tl, "bfs", "lva", 0, V, True, lev == 1 or not C["kd"])
+        if lev == 1 or not C["kd"]:
+            lin("lvs" + n, S("lvs", 0, 96), tl, 1.0, 0.0)
+        else:
+            squeeze("lvr2", tl, "bfs", "lvb", 0, V, False, True)
+            relu("lvt2", S("lvs", 0, 96), tl, 1.0)
+        for k in (1, 0):
+            xb = lst("xb", k)
+            if lev == 1:
+                tl = tile(LW)
+                mm("sw1", tl, [(I("i1"), lst(qq, 2 * k + 1)), (I("im1"), lst(qq, 2 * k))])
+                tt("xb1", xb, tl, S("cc", 0, LW), ALU.mult)
+            td, tx = tile(240), tile(240)
+            for h in (0, 1):
+                j = 2 * k + h
+                mm("to" + n, lst(td[0], h), [(I("i1"), lst(qq, j)), (I("im1"), lst("id16", j))] + ([(I("fm1" if h else "f1"), xb)] if lev == 1 else []))
+            for h in (0, 1):
+                tt("xa" + n, lst(tx[0], h), lst(td[0], h), S("lvs", 0, LW), ALU.mult)
+            f = S("ff", 240 * k, 240 * k + 240)
+            tt("ff" + n, f, tx, S("idf", 240 * k, 240 * k + 240), ALU.add)
+            if lev == 1:
+                dma("lw1", row("lw", 1 - k), f, RB)
+        lin("ul" + n, S("ul" + n, 0, 480), S("ff", 0, 480), 0.5, -0.25)
+        if lev == 2:
+            tt("lc2", S("cc", 0, 96), S("cc", 0, 96), S("lvs", 0, 96), ALU.mult)
+            tl, tx = tile(LW), tile(LW)
+            mm("sw2", tl, [(I("i1"), lst(qq, 3)), (I("im1"), lst(qq, 2))])
+            tt("xb2", tx, tl, S("cc", 0, LW), ALU.mult)
+            tt("fa2", lst("xb", 0), lst("ff", 2), tx, ALU.add)
+            tt("fb2", lst("xb", 1), lst("ff", 3), tx, ALU.subtract)
+            dma("lw2", row("lw", 0), S("xb", 0, 240), RB)
+        own, hg, PK = ("hh" if lev == 1 else "w2"), "hg" + n, S("pk" if lev == 1 else "pki", 0, W)
+        for i, (lo, hi, mode) in enumerate([(V, W, "C")] + [x + (C["s1d"],) for x in C["s1"]] if lev == 1 else C["s2"]):
+            o, g = (S(hg, lo - V, hi - V), "g") if lo >= V else (S(own, lo, hi), "")
+            if mode == "T":
+                tl, parts = tile(hi - lo), [S("gg", 2048 * (i % 2) + 512 * j, 2048 * (i % 2) + 512 * j + hi - lo) for j in range(4)]
                 for j in range(4):
-                    gat("sp" + n, S("gg", W * j + lo, W * j + hi), PK, lst(nd, j, lo, hi))
-                for j in range(4):
-                    mm("sm" + n, tl, [(I("i1"), S("gg", W * j + lo, W * j + hi))], j == 0, j == 3)
-                if plain:
-                    lin("se" + n, o, tl, 1.0, 0.0)
-                else:
-                    tt("se" + n, o, tl, S("xw2", lo, hi), ALU.add)
+                    gat("sp2" + g, parts[j], PK, lst(nd, j, lo, hi))
+                mm("sm2" + g, tl, [(I("i1"), x) for x in parts])
+                lin("se2" + g, o, tl, 1.0, 0.0)
+            elif mode == "D":
+                b = S("z2", lo, hi)
+                gat("sa1", o, PK, lst(nd, 0, lo, hi))
+                gat("sb1", b, PK, lst(nd, 1, lo, hi))
+                gop("sc1", o, PK, lst(nd, 2, lo, hi), o, ALU.add)
+                gop("sd1", b, PK, lst(nd, 3, lo, hi), b, ALU.add)
+            else:
+                gat("sa" + n + g, o, PK, lst(nd, 0, lo, hi))
+                for j in (1, 2, 3):
+                    gop("sc" + n + g, o, PK, lst(nd, j, lo, hi), o, ALU.add)
             if hi == W:
                 exchange(2 * lev - 1, hg, "rc" + n, 0, -1)
-        for lo, hi in OWN:
-            tl = tile("kl", hi - lo)
-            mm("kl" + n, tl, [(I("imh"), S("ones", 0, hi - lo)), (I("imh"), S("sg", lo, hi))])
-            tt("h" + n, S("h" + n, lo, hi), tl, S("d32", lo, hi), ALU.mult)
         for d in range(3):
-            blk, tm = S("shu", 8 * d, 8 * d + 8), S("tm", NB * d, NB * d + NB)
-            gop("home" + n, tm, S(own, 0, V), blk, S("rc" + n, NB * d, NB * d + NB), ALU.add)
-            sca("homes" + n, S(own, 0, V), blk, tm)
-        gat("out" + n, S("s" + n, 0, GH), S(own, 0, V), SH)
+            blk, o = S("shu", 8 * d, 8 * d + 8), S("tm" if lev == 2 and d < 2 else "s2", NB * d, NB * d + NB)
+            gop("home" + n, o, S(own, 0, V), blk, S("rc" + n, NB * d, NB * d + NB), ALU.add)
+            sca("homes" + n, S(own, 0, V), blk, o)
+        if lev == 1:
+            if C["s1d"] == "D":
+                gop("outa1", S("tm", 0, GH), S("z2", 0, V), SH, S("s0", 0, GH), ALU.add)
+            gop("outb1", S("s1", 0, GH), S("hh", 0, V), SH, S("tm" if C["s1d"] == "D" else "s0", 0, GH), ALU.add)
+        else:
+            gat("out2", S("s2", 0, 2 * NB), S("w2", 0, V), S("shu", 0, 16))
         exchange(2 * lev, "s" + n, own, V, 1)
 
+    for lo, hi in T4 + [(V, W)]:
+        copy("x161", S("x16", lo, hi), S("xi", lo, hi))
     level(1)
     for j in (2, 3, 0, 1):
         for lo, hi in C["lp"]:
-            gat("lk", S("ab", W * j + lo, W * j + hi), S("lw", 0, 2 * W), lst("ps1", j, lo, hi), -1920.0)
-        tl = tile("D", LW)
-        squeeze("lq", tl, "bp0" if j >= 2 else "bp1", "ab", W * j, W)
+            gat("lk", S("rr", W * j + lo, W * j + hi), S("lw", 0, 2 * W), lst("ps1", j, lo, hi), -1920.0)
+        tl = tile(LW)
+        squeeze("lq", tl, "bp0" if j >= 2 else "bp1", "rr", W * j, W)
         lin("nd2", lst("nd2", j), tl, 0.5, 959.75)
         lin("q2", lst("q2", j), tl, 1.0, 0.0)
-    for lo, hi in C["ec"]:
-        tl, h, r = tile("xh", hi - lo), S("hh", lo, hi), S("r16", lo, hi)
-        ts("r16", r, h, MAGIC, MAGIC, ALU.add, ALU.subtract)
-        mm("xh", tl, [(I("f2k"), h)], True, False)
-        mm("xr", tl, [(I("im2047"), r), cst(2, hi - lo)], False, True)
-        tt("xw2", S("xw2", lo, hi), tl, S("xi", lo, hi), ALU.add)
+    for lo, hi in OWN:
+        tl = tile(hi - lo)
+        mm("xn2", tl, [(I("i1"), S("x16", lo, hi))] + ([(I("f1"), S("z2", lo, hi))] if C["s1d"] == "D" else []), True, False)
+        mm("xm2", tl, [(I("f1"), S("hh", lo, hi))], False, True)
+        lin("xe2", S("xw2", lo, hi), tl, 1.0, 0.0)
+        tt("r16", S("r16", lo, hi), tl, S("xw2", lo, hi), ALU.subtract)
+    lin("xg2", S("xw2", V, W), S("hh", V, W), 1.0, 0.0)
+    for lo, hi in OWN + [(V, W)]:
+        copy("x162", S("x16", lo, hi), S("xw2", lo, hi))
     level(2)
     lin("b2", S("b16", 240, 480), S("q2", 240, 480), 1.0 / 32, 1090 - 31.0 / 64)
     positions("ps2", S("ps2", 0, 240), S("q2", 240, 480), S("b16", 240, 480))
@@ -421,33 +512,65 @@ def build(C):
     dma("st_yn", ("yn", 0, 0), row("z1"), RB)
 
     def undo(lev, win, lo, hi, mode):
-        ul, m, t, t2 = "ul%d" % lev, hi - lo, S("t", lo, hi), S("hh", lo, hi)
-        tl, rnd = tile("um", m), ([] if lev == 2 else [cst(0, m), cst(1, m)])
-        gat("ug", t, win, lst(ul, 0, lo, hi), -3.0 if lev == 2 else -1.5)
-        first = [(I("im1"), S("h%d" % lev, lo, hi))] + ([(I("im1"), S("r16", lo, hi))] if lev == 2 else [])
-        if mode == "dbl":
-            gat("ug", t2, win, lst(ul, 1, lo, hi))
-            gop("uc", t, win, lst(ul, 2, lo, hi), t, ALU.add)
-            gop("uc", t2, win, lst(ul, 3, lo, hi), t2, ALU.add)
-            mm("um", tl, first + [(I("fq"), t)], True, False)
-            mm("um", tl, [(I("fq"), t2)] + rnd, False, True)
+        n, m = "%d" % lev, hi - lo
+        ul, t, t2 = "ul" + n, S("t" if lev == 2 else "pk", lo, hi), S("kw" if lev == 2 else "hh", lo, hi)
+        tl, rnd = tile(m), ([] if lev == 2 or lo in C["yv"] else [cst(0, m), cst(1, m)])
+        gat("ug" + n, t, win, lst(ul, 0, lo, hi), -1.5)
+        if lev == 2:
+            mm("ua", tl, [(I("im16k"), S("r16", lo, hi)), (I("im1"), S("h2", lo, hi))], True, False)
+            mm("ub", tl, [(I("i1"), S("d16", lo, hi))] + combo(lo, hi, [0.25] * 4), False, False)
+        first = [] if lev == 2 else [(I("i16k"), S("h1", lo, hi))]
+        if mode == "D":
+            gat("ug" + n, t2, win, lst(ul, 1, lo, hi))
+            gop("uc" + n, t, win, lst(ul, 2, lo, hi), t, ALU.add)
+            gop("uc" + n, t2, win, lst(ul, 3, lo, hi), t2, ALU.add)
+            mm("um" + n, tl, first + [(I("fq"), t)], lev == 1, False)
+            mm("um" + n, tl, [(I("fq"), t2)] + rnd, False, True)
         else:
             for j in (1, 2, 3):
-                gop("uc", t, win, lst(ul, j, lo, hi), t, ALU.add)
-            mm("um", tl, first, True, False)
-            mm("um", tl, [(I("fq"), t)] + rnd, False, True)
+                gop("uc" + n, t, win, lst(ul, j, lo, hi), t, ALU.add)
+            mm("um" + n, tl, first + [(I("fq"), t)] + rnd, lev == 1, True)
         return tl
 
-    tl = tile("um", GH)
-    mm("wg", tl, [(I("im1"), S("r16", V, W)), (I("f1"), S("w2", V, W))])
-    lin("w1g", S("d32", V, W), tl, 1.0, 0.0)
-    for lo, hi, mode in C["u2"]:
-        lin("w1", S("d32", lo, hi), undo(2, S("w2", 0, W), lo, hi, mode), 1.0, 0.0)
-    for lo, hi, mode in C["u1"]:
-        y = S("z2", 2048 + lo, 2048 + hi)
-        lin("y", y, undo(1, S("d32", 0, W), lo, hi, mode), 1.0, 0.0)
+    tl = tile(GH)
+    mm("wa", tl, [(I("fm16k"), S("hh", V, W)), (I("i16k"), S("x16", V, W)), (I("i1"), S("x16", V, W))], True, False)
+    mm("wg", tl, [(I("f1"), S("w2", V, W))], False, True)
+    lin("w1g", S("xw2", V, W), tl, 1.0, 0.0)
+    for (lo, hi), mode in zip(T4, C["u2"]):
+        lin("w1", S("xw2", lo, hi), undo(2, S("w2", 0, W), lo, hi, mode), 1.0, 0.0)
+    for (lo, hi), mode in zip(T4, C["u1"]):
+        y, tl = S("z2", 2048 + lo, 2048 + hi), undo(1, S("xw2", 0, W), lo, hi, mode)
+        if lo in C["yv"]:
+            ts("y", y, tl, MAGIC, MAGIC, ALU.add, ALU.subtract)
+        else:
+            lin("y", y, tl, 1.0, 0.0)
         dma("st_x", ("yx", lo, hi), y, 512 * (hi - lo))
     return ops
+
+
+def arrange(ops):
+    at, seen, calls = {}, {}, {}
+    for k, o in enumerate(ops):
+        seen[o["name"]] = seen.get(o["name"], -1) + 1
+        at["%s.%d" % (o["name"], seen[o["name"]])] = at[o["name"]] = k
+        for t in o["tiles"]:
+            calls.setdefault(t, []).append(k)
+    seq, eng, extra, idle = [], {}, {}, [(b, None) for b in range(8)]
+    for x in ORDER.split():
+        name, _, e = x.partition("/")
+        k = at[name]
+        seq.append(k)
+        eng[k] = e or list(ops[k]["impl"])[0]
+        for t in ops[k]["tiles"]:
+            if calls[t][0] == k:
+                BANK[t], last = idle.pop(0)
+                if last is not None:
+                    extra[k] = last
+        for t in sorted(ops[k]["tiles"], key=lambda t: calls[t][0]):
+            if calls[t][-1] == k:
+                idle.append((BANK[t], k))
+    assert sorted(seq) == list(range(len(ops)))
+    return {"eng": eng, "seq": seq, "extra": extra, "order": {e: [k for k in seq if eng[k] == e] for e in "vapgsx"}}
 
 
 def plan(ops, sc):
@@ -455,13 +578,11 @@ def plan(ops, sc):
     pos = {k: i for e in order for i, k in enumerate(order[e])}
     keep, marked, count = {e: [] for e in order}, set(), {}
     for e in order:
-        seen, prev = {}, None
+        seen = {}
         for k in order[e]:
             last, deps = {}, set(ops[k]["deps"])
-            if e == "g" and not ops[k].get("send"):
-                if prev is not None and "nb1" in (ops[k]["name"], ops[prev]["name"]):
-                    deps.add(prev)
-                prev = k
+            if k in sc["extra"]:
+                deps.add(sc["extra"][k])
             for j in deps:
                 if e == "x" or ops[j].get("send") or (e == "p" and eng[j] == "p"):
                     continue
@@ -484,14 +605,12 @@ def plan(ops, sc):
 
 
 CACHE = {}
-DIGITS = "0123456789abcdefghijklmnopqrstuvwxyzABCDEFGHIJKLMNOPQRSTUVWXYZ"
 
 
 def program():
     if "p" not in CACHE:
         ops = build(CFG)
-        seq = [DIGITS.index(ORDER[i]) * 62 + DIGITS.index(ORDER[i + 1]) for i in range(0, len(ORDER), 2)]
-        sc = {"eng": QUEUE, "order": {e: [k for k in seq if QUEUE[k] == e] for e in "vapgsx"}}
+        sc = arrange(ops)
         CACHE["p"] = (ops, sc) + plan(ops, sc)
     return CACHE["p"]
 

from concourse.bass import DstId, RemoteDMATransfer
from concourse.mybir import AluOpType, ActivationFunctionType

ALU = AluOpType
FN = ActivationFunctionType
V, W, GH, NB, LW = 1536, 1920, 384, 128, 120
MAGIC = 12582912.0
EPS = 2.0 ** -14
OWN = [(0, 512), (512, 1024), (1024, V)]
T4 = [(0, 512), (512, 1024), (1024, 1408), (1408, V)]
CFG = {
    "na": 2016, "piece": 320,
    "xp": OWN + [(V, W)], "xc": T4[:2] + [(V, W)] + T4[2:], "lp": [(0, 960), (960, W)],
    "s1": [(0, 768), (768, V)],
    "s2": [(V, W, "T"), (0, 512, "T"), (512, 1024, "C"), (1024, V, "C")],
    "u2": "DDCC", "u1": "DCCC",
    "s1d": "D", "kd": True,
    "yv": (0, 512, 1024, 1408),
}
ORDER = """
pc zb zc ld_nxt z2row ones i1 zpki i16k/a znomay on pd im120/a z1row crow.3 ih/v im257/v lvs imh/a br/v ld_x ld_shw i4k/a shu/a pf/a oe idi border.0
ld_th qc/a iv0 prawm praw/a sca.0 scv.0 iv1 sca.1 idf s0/v scv.1 zlw.0 crow.1 send0 di.1 di.0 nw gt border.1 in13/v di.2 di.3 ie27/a pr16/a thn zpk
dei.0 x161.3 ie15/a dei.1 nd1n/a q1n/a arrive0 cc border.2 dei.2 dei.3 xo1.7/a imq/g x161.0 xo1.4/a crow.0 c1 bp0 c2 x161.2 blq xo1.1/v pi nd1p/a
xo1.0/v yb1.0 xd1.2 bt xo1.5/a xd1.0 yb1.1 ya1.1 xo1.3/a yb1.2 nb.1 xd1.1 bf ya1.0 anti xo1.6/a xo1.2/a xd1.3 xi1.0/a xi1.1/a rd1.3/a xd1.4 yc1.0 d1.0
x161.1 bl/a yb1.4 xd1.5 ps1n/a gs yb1.3 x161.4 ad1.0 nb.0 yc1.1 d1.1 fm1/a ya1.2 yc1.2 ad1.2 xd1.7 ya1.3 xd1.6 ad1.1 q1p/a bfn/a yc1.3 d1.2 ad1.3 e1.0
key1.0/v nb.2 kwz e1.2 ya1.4 yc1.4 nb.3 d1.3 key1.2/a ad1.4 nka1 e1.1 key1.1/v nkb1/a e1.3 nb.4 im16k/g key1.3/a e1.4 key1.4/v th0 rd1.4/v k1.0/a
im1/g crow.2 zlw.5 crow.4 thd u1.5 k1.1/a r1.5/v rd1.1/a iq/g u1.4 rd1.2/a r1.4/a kc1.0 bp1 kc1.1 u1.2 u1.3 r1.3/a kc1.3 kc1.2 rd1.0/a u1.1 r1.1/a
u1.0 kc1.4 r1.0/a lv1.0 zlw.1 fs1.0 zlw.2 k1.2/a kc1.6 zlw.3 rd1.5/a r1.2/a ma1.0 id16/a s1.3/a ma1.1 ma1.2 kc1.5 s1.2/a m1.0 ma1.3 b1p/a kc1.7 lv1.1
fs1.1 kl1.0/a k1.3/a fs1.2 m1.1 kc1.8 s1.1/a kc1.9 s1.0/a lv1.2 kl1.1/a kc1.10 kc1.11 lv1.3 n1.0 pk1.0 m1.2 n1.1 pk1.1 kl1.2/a m1.3 n1.2 pk1.2 zlw.6
kl1.3/a n1.3 pk1.3 fs1.3 sw1.0 bfs/a f1/v sw1.1 cc1 sa1g/a lvq1 xb1.0 to1.0 xb1.1 sb1.1/a sc1g.0 sc1g.1 zlw.7 lvs1/v sc1g.2 to1.1 xa1.0 to1.2 to1.3
xa1.2 zlw.4 o1.2 send1 arrive1 xa1.1 xa1.3 sb1.0/a ff1.0 lw1.0 ff1.1 ps1pm o1.1 sa1.0/a sd1.1 xn2.2 ps1p/a o1.0 sd1.0 xn2.1 sa1.1/a sc1.1 sc1.0 outa1
home1.0 homes1.0 o1.3 h1.3 xn2.0 home1.1 homes1.1 home1.2 homes1.2 lw1.1 outb1 lk.0/a lk.1/a lq.0 xm2.1 h1.0 send2 arrive2 h1.2 nd2.0/v lk.3/a lk.2/a
lq.1 xm2.0 h1.1 lk.7/v xm2.2 xe2.0/v nd2.1/v lk.4/a lk.5/a lq.2 xe2.1/a r16.1 r16.0 xg2/v x162.3 x162.1 lk.6/a lq.3 xe2.2/a xo2.1/v nd2.3/v x162.0
nd2.2/a xd2.2 q2.2/a nka2 q2.1/a xo2.0/v xo2.5/a xd2.3 xd2.0 yb2.1 xo2.2/a xo2.6/a ya2.1 xo2.4/a xd2.1 yb2.3 yb2.0 yc2.1 d2.1 xd2.4 ya2.0 xo2.3/a
xo2.7/a yb2.2 rs2.0 yc2.0 d2.0 xi2.1/a x162.2 xi2.0/a u2.3 ya2.2 yc2.2 xd2.5 ya2.3 r2.3 xd2.6 xd2.7 ad2.0 adc.0 yc2.3 d2.2 ad2.1 adc.1 rm2.0 yb2.4
ya2.4 yc2.4 ad2.2 d2.3 ad2.3 adc.3 e2.0 key2.0/a e2.1 e2.3 adc.2 e2.2 key2.1/v nkb2/a ad2.4 adc.4 e2.4 r16.2 key2.4/v q2.3/v ma2.1 key2.3/a key2.2/a
k2.0/v q2.0/a k2.3/a kd2.6 kb2.0/a k2.2/a kd2.0 k2.1/a u2.4 r2.4 kd2.4 lv2.0 rs2.1 kd2.1 u2.0 kd2.2 lb2.0 rs2.2 r2.0 u2.2 lv2.1 kb2.1/a kd2.3 ma2.2
ma2.0 lv2.2 m2.0 r2.2 lb2.1 ma2.3 kb2.2/a kd2.5 b2/a lv2.3 kb2.3/a kd2.7 ra2.0 m2.1 rs2.4 lb2.2 m2.2 h2.0 h2.1 ul1/a lb2.3 m2.3 h2.2 ua.0 pk2.0/a
pk2.1/a pk2.2/a h2.3 pk2.3/v sp2g.3/v sp2g.0/v ua.2 fq/a ps2m sp2g.1/a to2.2 sp2g.2/a sa2.1/a sa2.0/v sc2.0 ua.3 sm2g se2g/a to2.0 ub.0 to2.1 to2.3
sp2.2/a sp2.0/a sp2.1/a sp2.3/a ps2/a sc2.3 sc2.1 sc2.4 send3 arrive3 ub.2 u2.5 sm2 se2/a fm16k/a sc2.2 sc2.5 home2.0 homes2.0 home2.1 homes2.1 ub.3
r2.5 u2.1 ua.1 lvq2 lvr2 home2.2 rs2.5 homes2.2 rm2.1 lvt2/v xa2.0 xa2.1 ra2.2 rm2.2 xa2.2 ub.1 r2.1 ra2.5 out2/a send4 sw2 rs2.3 xa2.3 rm2.5 rm2.3
ra2.1 ra2.4 ra2.3 fs2.0 rm2.4 ff2.0 fs2.1 ff2.1 fs2.2 ul2/v arrive4 ug2.0/a fs2.3 wa ug2.1/a cc2 lc2 xb2 ug2.5/v uc2.7 wg ug2.2/a fa2 uc2.0 um2.0
ug2.4/a uc2.1 um2.1 ug2.3/a w1.0/a uc2.2 um2.2 uc2.4 uc2.3 um2.3 uc2.5 uc2.6 uc2.8 uc2.9 um2.4 w1g/v fb2 lw2 w1.1/a um2.5 w1.3/v w1.2/a ug1.1/v
ug1.0/a uc1.0 uc1.1 um1.0 ug1.3/a um1.1 ug1.2/a uc1.2 ug1.4/a uc1.8 uc1.3 uc1.5 yn.0/a uc1.4 um1.2 yn.2/a uc1.6 uc1.9 uc1.7 um1.3 y.0 st_x.0 y.1
st_x.1 uc1.10 y.2 yn.1/a um1.4 st_x.2 yn.3/a st_yn y.3 st_x.3
"""
I32, U16, F32, F16, B16 = "int32", "uint16", "float32", "float16", "bfloat16"
SB = {}
for _d, _l in ((I32, "nxi:240 shi:24 thi:4 xi:1920 xw2:1920 pki:1920 s0:384 pi:240 pc:4 pd:4"),
               (U16, "shu:24 nk:96 praw:240 nd1:480 nd2:480 ps1:480 ps2:240 ul1:480 ul2:480"),
               (F32, "thn:4 kw:1928 bl:96 nkf:96 t:1536 pk:1920 hh:1920 hg1:384 rc1:384 tm:384 s1:384 s2:384 w2:1920 z1:3840 z2:3840 "
                     "lw:3840 iv:2112 zc:240 c1:240 c2:240 idf:480 pf:4 lvs:120 cc:120 xb:240 ff:480 f1:128 fm1:128 fq:128 fm16k:128"),
               (F16, "ab:7680 gg:4096 nb:1920 d16:1536 ad:1920 adc:1920 lva:1536 lvb:1536 hg2:384 rc2:384 rr:7680 h1:1536 h2:1536 "
                     "r16:1536 x16:1920 qc:240 br:240 b16:480 pr16:240 q1:480 q2:480 id16:480 im257:128 thd:128 th0:128"),
               (B16, "nomay:1536 ones:512 oe:512 on:512 zb:128 crow:640 nw:128 gs:128 gt:144 bt:144 bf:144 bfn:144 bfs:144 "
                     "bp0:144 bp1:144 di:512 anti:128 i1:128 im1:128 imq:128 imh:128 iq:128 ih:128 i4k:128 i16k:128 im16k:128 im120:128 "
                     "ie27:128 ie15:128 in13:128")):
    for _x in _l.split():
        SB[_x.split(":")[0]] = (int(_x.split(":")[1]), _d)
SCALED = {"im1": -1.0, "imq": -0.25, "imh": -0.5, "iq": 0.25, "ih": 0.5, "i4k": 4096.0, "i16k": 1 / EPS, "im16k": -1 / EPS,
          "im120": -120.0, "im257": -257.0, "ie27": EPS / 16384, "ie15": EPS / 2, "in13": -1.0 / 16384,
          "f1": 1.0, "fm1": -1.0, "fq": 0.25, "fm16k": -1 / EPS}
IDENT = {1.0: "i1", -1.0: "im1", -0.25: "imq", -0.5: "imh", 0.25: "iq", 0.5: "ih"}
SCRATCH = {k: ("sbuf", [128, n], d) for k, (n, d) in SB.items()}
for _k in range(8):
    SCRATCH["bank%d" % _k] = ("psum", [128, 512], F32)
SEMAPHORES = ["ev", "ea", "ep", "eg", "loc"] + ["ar%d" % k for k in range(5)] + ["dm%d" % k for k in range(20)]
BANK = {}


def S(buf, lo, hi, step=1, p=None):
    return (buf, lo, hi, step, p)


def width(r):
    return (r[2] - r[1] + r[3] - 1) // r[3]


def psum(r):
    return r[0][0] == "#"


def two(r):
    return (not psum(r)) and SB[r[0]][1] in (F16, B16, U16)


def ap(T, r):
    if isinstance(r, (int, float)):
        return r
    t = T["bank%d" % BANK[r[0]]] if psum(r) else T[r[0]]
    p = slice(0, 128) if r[4] is None else slice(r[4][0], r[4][1], r[4][2])
    return t[p, r[1]:r[2]] if r[3] == 1 else t[p, r[1]:r[2]:r[3]]


def build(C):
    ops, acc, ntile, ndma = [], {}, [0], [0]

    def meet(a, b):
        if a[1] >= b[2] or b[1] >= a[2]:
            return False
        return a[4] is None or b[4] is None or len(set(range(*a[4])) & set(range(*b[4]))) > 0

    def add(name, impl, reads, writes, **kw):
        k, deps, tiles = len(ops), set(), set()
        for r, wr in [(r, False) for r in reads if isinstance(r, tuple)] + [(r, True) for r in writes]:
            for (j, q, wq) in acc.get(r[0], [])[-2 if psum(r) else 0:]:
                if j != k and (psum(r) or ((wr or wq) and meet(r, q))):
                    deps.add(j)
            acc.setdefault(r[0], []).append((k, r, wr))
            if psum(r):
                tiles.add(r[0])
        ops.append(dict(kw, name=name, impl=impl, deps=deps, tiles=tiles))
        return k

    def tile(m):
        ntile[0] += 1
        return S("#%d" % ntile[0], 0, m)

    def vts(o, i, s1, s2, op0, op1=None):
        n = width(i) * (0.5 if two(o) and two(i) else 1)
        if op1 is None:
            return ("v", n, lambda q, T: q.tensor_scalar(ap(T, o), ap(T, i), ap(T, s1), None, op0))
        return ("v", n, lambda q, T: q.tensor_scalar(ap(T, o), ap(T, i), s1, s2, op0, op1))

    def aact(o, i, f, bias, scale):
        return ("a", width(i), lambda q, T: q.activation(ap(T, o), ap(T, i), f, bias=bias, scale=scale))

    def gsel(o, i, pat, op, fl, base, cm):
        return ("g", width(o), lambda q, T: q.affine_select(ap(T, o), ap(T, i), pat, op, fl, base, cm))

    def ts(name, o, i, s1, s2, op0, op1=None):
        add(name, {"v": vts(o, i, s1, s2, op0, op1)}, [i, s1], [o])

    def act(name, o, i, f, bias=0.0, scale=1.0):
        add(name, {"a": aact(o, i, f, bias, scale)}, [i], [o])

    def lin(name, o, i, scale, bias):
        add(name, {"v": vts(o, i, scale, bias, ALU.mult, ALU.add), "a": aact(o, i, FN.Identity, bias, scale)}, [i], [o])

    def relu(name, o, i, c):
        add(name, {"v": vts(o, i, c, c, ALU.max, ALU.subtract), "a": aact(o, i, FN.Relu, -c, 1.0)}, [i], [o])

    def copy(name, o, i):
        add(name, {"g": gsel(o, i, [[0, width(o)]], ALU.is_ge, 0.0, 0, 0)}, [i], [o])

    def tt(name, o, a, b, op):
        n = width(a) * (1 if psum(a) or psum(b) else 2)
        add(name, {"v": ("v", n, lambda q, T: q.tensor_tensor(ap(T, o), ap(T, a), ap(T, b), op))}, [a, b], [o])

    def ind(T, win, idx):
        return ap(T, win).indirect(ap(T, idx))

    def gat(name, o, win, idx, bias=0.0):
        def fv(q, T):
            if bias == 0.0:
                return q.tensor_copy(ap(T, o), ind(T, win, idx))
            return q.tensor_scalar(ap(T, o), ind(T, win, idx), bias, None, ALU.add)
        add(name, {"v": ("vg", width(o), fv),
                   "a": ("ag", width(o), lambda q, T: q.activation(ap(T, o), ind(T, win, idx), FN.Identity, bias=bias, scale=1.0))}, [win, idx], [o])

    def gop(name, o, win, idx, b, op):
        add(name, {"v": ("vg", width(o), lambda q, T: q.tensor_tensor(ap(T, o), ind(T, win, idx), ap(T, b), op))}, [win, idx, b], [o])

    def sca(name, win, idx, i):
        add(name, {"v": ("vs", width(i), lambda q, T: q.tensor_copy(ind(T, win, idx), ap(T, i)))}, [idx, i], [win])

    def mm(name, o, terms, start=True, stop=True):
        cyc = sum(max(64, width(r)) * (4 if SB[r[0]][1] == F32 else 1) for l, r in terms)

        def f(q, T):
            ins = None
            for k, (l, r) in enumerate(terms):
                ins = q.matmul(ap(T, o), ap(T, l), ap(T, r), start and k == 0, stop and k == len(terms) - 1)
            return ins
        add(name, {"p": ("p", cyc, f)}, [x for lr in terms for x in lr], [o])

    def I(name):
        return S(name, 0, 128)

    def cst(k, n):
        return (S("crow", 128 * k, 128 * k + 128, 1, (0, 1, 1)), S("ones", 0, n, 1, (0, 1, 1)))

    def fill(name, o, c):
        add(name, {"v": ("v", width(o) * (0.5 if two(o) else 1), lambda q, T: q.memset(ap(T, o), c))}, [], [o])

    def iota(name, o, pat, base, cm):
        kw = {} if SB[o[0]][1] == I32 else {"allow_small_or_imprecise_dtypes": True}
        add(name, {"g": ("g", width(o), lambda q, T: q.iota(ap(T, o), pat, base, cm, **kw))}, [], [o])

    def sel(name, n, src, pat, op, base, cm, lo=0):
        o, i = S(name, lo, lo + n), S(src, 0, n)
        add(name, {"g": gsel(o, i, pat, op, 0.0, base, cm)}, [i], [o])

    def dma(name, o, i, nbytes, eng="s"):
        out = o[0] in ("yx", "yn")
        ndma[0] += 1

        def f(q, T):
            dst = ap(T, o) if not out else (T[o[0]][:, o[1]:o[2]] if o[2] else T[o[0]][:])
            return q.dma_start(dst, T[i][:] if isinstance(i, str) else ap(T, i))
        add(name, {eng: ("dma", nbytes, f)}, [i], [] if out else [o], sem="dm%d" % (ndma[0] - 1), final=out)

    def exchange(k, src, dst, off, sign):
        s = add("send%d" % k, {"g": ("rem", 1 if k == 0 else 0, (k, src, dst, off, sign))}, [S(src, 0, GH)], [], send=True)
        a = add("arrive%d" % k, {"x": ("arr", 0, None)}, [], [S(dst, off, off + GH)], sem="ar%d" % k)
        ops[a]["deps"].add(s)

    def lst(buf, j, lo=0, hi=W):
        return S(buf, LW * j + lo // 16, LW * j + hi // 16)

    def row(buf, r=0):
        return S(buf, 0, 2 * W, 1, (r, 128, 16))

    def squeeze(name, o, mask, buf, lo, n, start=True, stop=True):
        mm(name, o, [(S(mask, 15 - i, 143 - i), S(buf, lo + i, lo + n, 16)) for i in range(16)], start, stop)

    POSC = 120.0 * 1920 + 3839.0 * 1030

    def positions(name, o, q, b):
        tl = tile(240)
        mm(name + "m", tl, [(I("im120"), q), (I("i4k"), b), (I("im257"), b)])
        lin(name, o, tl, -1.0, POSC)
        return tl

    RB, SH = 128 * 960, S("shu", 0, 24)
    dma("ld_nxt", S("nxi", 0, 240), "nxt", RB, "a")
    dma("ld_shw", S("shi", 0, 24), "shw", 128 * 96)
    dma("ld_x", S("xi", 0, V), "x0", 128 * V * 4)
    dma("ld_th", S("thi", 0, 1), "th", 128 * 64)
    fill("zb", I("zb"), 0.0)
    fill("zc", S("zc", 0, 240), 0.0)
    dma("z1row", row("z1"), S("zc", 0, 240), RB, "a")
    dma("z2row", row("z2"), S("zc", 0, 240), RB, "a")
    add("i1", {"g": gsel(I("i1"), I("zb"), [[-1, 128]], ALU.not_equal, 1.0, 0, 1)}, [I("zb")], [I("i1")])
    for k, c in SCALED.items():
        impl = {"v": vts(I(k), I("i1"), c, None, ALU.mult), "a": aact(I(k), I("i1"), FN.Identity, 0.0, c)}
        if SB[k][1] == B16:
            impl["g"] = gsel(I(k), I("zb"), [[-1, 128]], ALU.not_equal, c, 0, 1)
        add(k, impl, [I("i1"), I("zb")], [I(k)])
    NA, PC = C["na"], C["piece"]
    iota("iv0", S("iv", 0, PC), [[1, PC]], 64, 0)
    iota("iv1", S("iv", PC, max(NA, W)), [[1, max(NA, W) - PC]], 64 + PC, 0)
    fill("ones", S("ones", 0, 512), 1.0)
    fill("oe", S("oe", 0, 512), EPS / 16384)
    fill("on", S("on", 0, 512), -1.0 / 16384)
    for k, c in enumerate([MAGIC, -MAGIC, 0.375, MAGIC * EPS, -MAGIC * EPS]):
        fill("crow", cst(k, 1)[0], c)
    NW = S("nw", 0, 128, 1, (0, 1, 1))
    fill("nw", NW, 1.0 / 2048)
    fill("lvs", S("lvs", 96, LW), 0.0)
    fill("cc", S("cc", 96, LW), 0.0)
    for k in range(4):
        sel("di", 128, "ones", [[16, 8], [1000, 2], [2, 8]], ALU.is_equal, k // 2 - 1000 * (k % 2), -1, 128 * k)
    sel("gt", 128, "ones", [[-16, 8], [0, 16]], ALU.is_ge, 0, 1)
    sel("gs", 128, "gt", [[16, 8], [0, 16]], ALU.is_ge, 15, -1)
    sel("bt", 144, "ones", [[16, 9], [1000, 16]], ALU.is_ge, 15 - 15000, -1)
    sel("bf", 144, "bt", [[-16, 9], [0, 16]], ALU.is_ge, 0, 1)
    for name, c in (("bfn", -1.0), ("bfs", 1.0 / 16)):
        lin(name, S(name, 0, 144), S("bf", 0, 144), c, 0.0)
    for r in range(2):
        sel("bp%d" % r, 144, "ones", [[16, 9], [1000, 16]], ALU.is_equal, r - 15000, -1)
    for lo, hi in C["xc"]:
        copy("nb", S("nb", lo, hi, 1, (0, 32, 1)), S("iv", lo, hi, 1, (0, 32, 1)))
    fill("znomay", S("nomay", 0, V), 0.0)
    fill("zpk", S("pk", V, W), 0.0)
    fill("zpki", S("pki", V, W), 0)
    for lo in range(0, 2 * W, 480):
        iota("zlw", S("lw", lo, lo + 480), [[0, 480]], 0, 0)
    ID = S("idf", 0, 480)
    iota("idi", ID, [[0, 2], [1, 2], [32, LW]], 0, 0)
    iota("pc", S("pc", 0, 1), [[0, 1]], 0, 2)
    ts("pd", S("pd", 0, 1), S("pc", 0, 1), 31, None, ALU.bitwise_and)
    lin("pf", S("pf", 0, 1), S("pd", 0, 1), 1.0, 0.0)
    ts("idf", ID, ID, S("pf", 0, 1), None, ALU.add)
    lin("id16", S("id16", 0, 480), ID, 1.0, -1920.0)
    ts("thn", S("thn", 0, 1), S("thi", 0, 1), 2047.0, -1.0, ALU.min, ALU.mult)
    ts("th0", I("th0"), I("i1"), S("thn", 0, 1), None, ALU.mult)
    add("anti", {"g": gsel(I("anti"), I("zb"), [[1, 128]], ALU.not_equal, 0.5, -127, 1)}, [I("zb")], [I("anti")])
    tt("thd", I("thd"), I("th0"), I("anti"), ALU.add)

    lin("shu", SH, S("shi", 0, 24), 1.0, 0.0)
    gat("s0", S("s0", 0, GH), S("xi", 0, V), SH)
    exchange(0, "s0", "xi", V, 1)

    lin("qc", S("qc", 0, 240), S("nxi", 0, 240), 1.0, -1920.0)
    lin("br", S("br", 0, 240), S("nxi", 0, 240), 1.0 / 32, 1030 - 31.0 / 64)
    tl = positions("praw", S("praw", 0, 240), S("qc", 0, 240), S("br", 0, 240))
    lin("pr16", S("pr16", 0, 240), tl, -1.0, POSC - 1920)

    def scatter(eng, lo, hi):
        idx = S("praw", lo // 16, hi // 16)
        if eng == "a":
            z, i = S("z2", 0, 2 * W), S("iv", lo, hi)
            add("sca", {"a": ("as1" if lo == 0 else "as", hi - lo, lambda q, T: q.activation(ind(T, z, idx), ap(T, i), FN.Silu))}, [idx, i], [z])
        else:
            z, i = S("z1", 0, 2 * W), S("iv", 0, hi - lo)
            add("scv", {"v": ("vs", hi - lo, lambda q, T: q.tensor_scalar(ind(T, z, idx), ap(T, i), 1.0, float(lo), ALU.mult, ALU.add))}, [idx, i], [z])
    scatter("a", 0, PC)
    scatter("a", PC, NA)
    scatter("v", NA, NA + PC)
    scatter("v", NA + PC, 2 * W)
    dma("c1", S("c1", 0, 240), row("z1"), RB)
    dma("c2", S("c2", 0, 240), row("z2"), RB)
    for src in ("qc", "pr16"):
        tl = tile(240)
        for j in range(2):
            mm("dei", lst(tl[0], j), [(S("di", 128 * (2 * j + h), 128 * (2 * j + h) + 128), S(src, h, 240, 2)) for h in range(2)])
        if src == "qc":
            lin("nd1n", S("nd1", 240, 480), tl, 0.5, 959.75)
            lin("q1n", S("q1", 240, 480), tl, 1.0, 0.0)
        else:
            lin("ps1n", S("ps1", 240, 480), tl, 1.0, 1920.0)
    PI = S("pi", 0, 240)
    tt("pi", PI, S("c1", 0, 240), S("c2", 0, 240), ALU.add)
    lin("nd1p", S("nd1", 0, 240), PI, 0.5, -32.25)
    lin("q1p", S("q1", 0, 240), PI, 1.0, -1984.0)
    lin("b1p", S("b16", 0, 240), PI, 1.0 / 32, 1028 - 31.0 / 64)
    positions("ps1p", S("ps1", 0, 240), S("q1", 0, 240), S("b16", 0, 240))
    for d in range(3):
        sca("border", S("nomay", 0, V), S("shu", 8 * d, 8 * d + 8), S("ones", 0, NB))
    tl = tile(96)
    squeeze("blq", tl, "bp0", "nomay", 0, V)
    lin("bl", S("bl", 0, 96), tl, 3840.0, -1920.0)
    fill("kwz", S("kw", W, W + 8), -1.0)

    def nbr(j, lo, hi):
        return S("ab", W * j + lo, W * j + hi)

    def combo(lo, hi, co):
        co = list(co)
        for j in (0, 1):
            if lo < V:
                co[2 + j] += co[j]
        return [(I(IDENT[co[j]]), nbr(j, lo, hi)) for j in range(4) if co[j]]

    def level(lev):
        n = "%d" % lev
        win, nd, qq, size = ("xi" if lev == 1 else "xw2"), "nd" + n, "q" + n, ("ad" if lev == 1 else "adc")
        beta, keys = (0.75 if lev == 1 else 0.0), {}
        for j in (2, 3):
            for lo, hi in C["xp"]:
                gat("xo" + n, nbr(j, lo, hi), S(win, 0, W), lst(nd, j, lo, hi), -beta)
        for lo, hi in C["xc"]:
            for j in (0, 1):
                if lo < V:
                    gop("xd" + n, nbr(j, lo, hi), S(win, 0, W), lst(nd, j, lo, hi), nbr(2 + j, lo, hi), ALU.subtract)
                else:
                    gat("xi" + n, nbr(j, lo, hi), S(win, 0, W), lst(nd, j, lo, hi))
        for lo, hi in C["xc"]:
            m, tl, d = hi - lo, tile(hi - lo), S("d16", lo, hi)
            c = combo(lo, hi, [-0.25] * 4)
            mm("yb" + n, tl, c[2:] + ([cst(2, m)] if lev == 2 else []), True, False)
            mm("ya" + n, tl, c[:1], False, False)
            mm("yc" + n, tl, c[1:2] + [(I("i1"), S("x16", lo, hi))] + ([] if lo < V else [cst(0, m), cst(1, m)]), False, True)
            if lo < V:
                ts("d" + n, d, tl, MAGIC, MAGIC, ALU.add, ALU.subtract)
            act("ad" + n, S("ad", lo, hi), d if lo < V else tl, FN.Abs)
            if lev == 2:
                ts("adc", S("adc", lo, hi), S("ad", lo, hi), 255.0, None, ALU.min)
            keys[lo] = tile(m)
            mm("e" + n, keys[lo], [(NW, S("nb", lo, hi, 1, (0, 1, 1))), (I("gs"), S(size, lo, hi))])
            lin("key" + n, S("kw", lo, hi), keys[lo], 1.0, 0.0)
        tt("nka" + n, S("nkf", 0, 96), S(qq, 0, 96), S("bl", 0, 96), ALU.max)
        lin("nkb" + n, S("nk", 0, 96), S("nkf", 0, 96), 0.5, 959.75)
        slots = []
        for a, b in ((0, 2), (1, 3), (0, 3), (1, 2)):
            k, straight = len(slots), b == a + 2
            slots.append("bf" if lev == 1 and not straight else "bfn")
            for lo, hi in OWN:
                r, u = S("rr", V * k + lo, V * k + hi), nbr(a, lo, hi)
                if not straight:
                    u = tile(hi - lo)
                    mm("u" + n, u, combo(lo, hi, [1.0 if j == a else -1.0 if j == b else 0 for j in range(4)]))
                if lev == 1:
                    relu("rd1" if straight else "r1", r, u, beta)
                elif straight:
                    act("rs2", r, u, FN.Abs)
                    ts("rm2", r, r, 255.0, None, ALU.min)
                else:
                    act("r2", r, u, FN.Abs)
                    act("ra2", r, r, FN.Relu, 255.0, -1.0)
        for lo, hi in T4:
            t, t2, KW = S("t", lo, hi), S("w2", lo, hi), S("kw", 0, W)
            gat("k" + n, t, S("kw", 0, W + 8), lst("nk", 0, lo, hi))
            if lev == 1 or not C["kd"]:
                for j in (1, 2, 3):
                    gop("kc" + n, t, KW, lst(nd, j, lo, hi), t, ALU.min)
            else:
                gat("kb2", t2, KW, lst(nd, 1, lo, hi))
                gop("kd2", t, KW, lst(nd, 2, lo, hi), t, ALU.min)
                gop("kd2", t2, KW, lst(nd, 3, lo, hi), t2, ALU.min)
        for lo, hi in T4:
            m, d, l, h = hi - lo, S("d16", lo, hi), S("lva", lo, hi), S("h" + n, lo, hi)
            tt("lv" + n, l, keys[lo], S("t", lo, hi), ALU.is_lt)
            tl = tile(m)
            if lev == 1:
                s = S("pki", lo, hi)
                lin("s1", s, d, 0.25, -0.375)
                far, kept = [(I("thd"), S("oe", 0, m)), (I("ie27"), S("ad", lo, hi))], [(I("ie15"), l), cst(3, m), cst(4, m)]
                kl = S("lvb", lo, hi)
                mm("ma1", tl, far, True, False)
                mm("m1", tl, kept, False, True)
                lin("kl1", kl, tl, 1.0, 0.0)
                tl = tile(m)
                mm("n1", tl, [(I("i1"), l), (I("i1"), kl)])
                tt("pk1", S("pk", lo, hi), tl, s, ALU.mult)
                tl = tile(m)
                mm("o1", tl, [(I("i1"), kl)])
                tt("h1", h, tl, d, ALU.mult)
            else:
                l2 = S("lvb", lo, hi)
                if C["kd"]:
                    tt("lb2", l2, keys[lo], S("w2", lo, hi), ALU.is_lt)
                mm("ma2", tl, [(I("thd"), S("on", 0, m)), (I("in13"), S("ad", lo, hi))], True, False)
                mm("m2", tl, ([(I("iq"), l), (I("iq"), l2)] if C["kd"] else [(I("ih"), l)]) + [cst(0, m), cst(1, m)], False, True)
                tt("h2", h, tl, d, ALU.mult)
                lin("pk2", S("pki", lo, hi), h, 0.25, -0.375)
        tf = tile(96)
        for k, mask in enumerate(slots):
            squeeze("fs" + n, tf, mask, "rr", V * k, V, k == 0, k == len(slots) - 1)
        ts("cc" + n, S("cc", 0, 96), tf, 0.0 if lev == 1 else -2 * 16 * 255.0, None, ALU.is_lt)
        tl = tile(96)
        squeeze("lvq" + n, tl, "bfs", "lva", 0, V, True, lev == 1 or not C["kd"])
        if lev == 1 or not C["kd"]:
            lin("lvs" + n, S("lvs", 0, 96), tl, 1.0, 0.0)
        else:
            squeeze("lvr2", tl, "bfs", "lvb", 0, V, False, True)
            relu("lvt2", S("lvs", 0, 96), tl, 1.0)
        for k in (1, 0):
            xb = lst("xb", k)
            if lev == 1:
                tl = tile(LW)
                mm("sw1", tl, [(I("i1"), lst(qq, 2 * k + 1)), (I("im1"), lst(qq, 2 * k))])
                tt("xb1", xb, tl, S("cc", 0, LW), ALU.mult)
            td, tx = tile(240), tile(240)
            for h in (0, 1):
                j = 2 * k + h
                mm("to" + n, lst(td[0], h), [(I("i1"), lst(qq, j)), (I("im1"), lst("id16", j))] + ([(I("fm1" if h else "f1"), xb)] if lev == 1 else []))
            for h in (0, 1):
                tt("xa" + n, lst(tx[0], h), lst(td[0], h), S("lvs", 0, LW), ALU.mult)
            f = S("ff", 240 * k, 240 * k + 240)
            tt("ff" + n, f, tx, S("idf", 240 * k, 240 * k + 240), ALU.add)
            if lev == 1:
                dma("lw1", row("lw", 1 - k), f, RB)
        lin("ul" + n, S("ul" + n, 0, 480), S("ff", 0, 480), 0.5, -0.25)
        if lev == 2:
            tt("lc2", S("cc", 0, 96), S("cc", 0, 96), S("lvs", 0, 96), ALU.mult)
            tl, tx = tile(LW), tile(LW)
            mm("sw2", tl, [(I("i1"), lst(qq, 3)), (I("im1"), lst(qq, 2))])
            tt("xb2", tx, tl, S("cc", 0, LW), ALU.mult)
            tt("fa2", lst("xb", 0), lst("ff", 2), tx, ALU.add)
            tt("fb2", lst("xb", 1), lst("ff", 3), tx, ALU.subtract)
            dma("lw2", row("lw", 0), S("xb", 0, 240), RB)
        own, hg, PK = ("hh" if lev == 1 else "w2"), "hg" + n, S("pk" if lev == 1 else "pki", 0, W)
        for i, (lo, hi, mode) in enumerate([(V, W, "C")] + [x + (C["s1d"],) for x in C["s1"]] if lev == 1 else C["s2"]):
            o, g = (S(hg, lo - V, hi - V), "g") if lo >= V else (S(own, lo, hi), "")
            if mode == "T":
                tl, parts = tile(hi - lo), [S("gg", 2048 * (i % 2) + 512 * j, 2048 * (i % 2) + 512 * j + hi - lo) for j in range(4)]
                for j in range(4):
                    gat("sp2" + g, parts[j], PK, lst(nd, j, lo, hi))
                mm("sm2" + g, tl, [(I("i1"), x) for x in parts])
                lin("se2" + g, o, tl, 1.0, 0.0)
            elif mode == "D":
                b = S("z2", lo, hi)
                gat("sa1", o, PK, lst(nd, 0, lo, hi))
                gat("sb1", b, PK, lst(nd, 1, lo, hi))
                gop("sc1", o, PK, lst(nd, 2, lo, hi), o, ALU.add)
                gop("sd1", b, PK, lst(nd, 3, lo, hi), b, ALU.add)
            else:
                gat("sa" + n + g, o, PK, lst(nd, 0, lo, hi))
                for j in (1, 2, 3):
                    gop("sc" + n + g, o, PK, lst(nd, j, lo, hi), o, ALU.add)
            if hi == W:
                exchange(2 * lev - 1, hg, "rc" + n, 0, -1)
        for d in range(3):
            blk, o = S("shu", 8 * d, 8 * d + 8), S("tm" if lev == 2 and d < 2 else "s2", NB * d, NB * d + NB)
            gop("home" + n, o, S(own, 0, V), blk, S("rc" + n, NB * d, NB * d + NB), ALU.add)
            sca("homes" + n, S(own, 0, V), blk, o)
        if lev == 1:
            if C["s1d"] == "D":
                gop("outa1", S("tm", 0, GH), S("z2", 0, V), SH, S("s0", 0, GH), ALU.add)
            gop("outb1", S("s1", 0, GH), S("hh", 0, V), SH, S("tm" if C["s1d"] == "D" else "s0", 0, GH), ALU.add)
        else:
            gat("out2", S("s2", 0, 2 * NB), S("w2", 0, V), S("shu", 0, 16))
        exchange(2 * lev, "s" + n, own, V, 1)

    for lo, hi in T4 + [(V, W)]:
        copy("x161", S("x16", lo, hi), S("xi", lo, hi))
    level(1)
    for j in (2, 3, 0, 1):
        for lo, hi in C["lp"]:
            gat("lk", S("rr", W * j + lo, W * j + hi), S("lw", 0, 2 * W), lst("ps1", j, lo, hi), -1920.0)
        tl = tile(LW)
        squeeze("lq", tl, "bp0" if j >= 2 else "bp1", "rr", W * j, W)
        lin("nd2", lst("nd2", j), tl, 0.5, 959.75)
        lin("q2", lst("q2", j), tl, 1.0, 0.0)
    for lo, hi in OWN:
        tl = tile(hi - lo)
        mm("xn2", tl, [(I("i1"), S("x16", lo, hi))] + ([(I("f1"), S("z2", lo, hi))] if C["s1d"] == "D" else []), True, False)
        mm("xm2", tl, [(I("f1"), S("hh", lo, hi))], False, True)
        lin("xe2", S("xw2", lo, hi), tl, 1.0, 0.0)
        tt("r16", S("r16", lo, hi), tl, S("xw2", lo, hi), ALU.subtract)
    lin("xg2", S("xw2", V, W), S("hh", V, W), 1.0, 0.0)
    for lo, hi in OWN + [(V, W)]:
        copy("x162", S("x16", lo, hi), S("xw2", lo, hi))
    level(2)
    lin("b2", S("b16", 240, 480), S("q2", 240, 480), 1.0 / 32, 1090 - 31.0 / 64)
    positions("ps2", S("ps2", 0, 240), S("q2", 240, 480), S("b16", 240, 480))
    for j, h in ((0, 0), (1, 1), (1, 0), (0, 1)):
        lo, hi = 960 * h, 960 * h + 960
        gat("yn", S("z1", 2 * lo + j, 2 * hi, 2), S("lw", 0, 2 * W), lst("ps2", j, lo, hi))
    dma("st_yn", ("yn", 0, 0), row("z1"), RB)

    def undo(lev, win, lo, hi, mode):
        n, m = "%d" % lev, hi - lo
        ul, t, t2 = "ul" + n, S("t" if lev == 2 else "pk", lo, hi), S("kw" if lev == 2 else "hh", lo, hi)
        tl, rnd = tile(m), ([] if lev == 2 or lo in C["yv"] else [cst(0, m), cst(1, m)])
        gat("ug" + n, t, win, lst(ul, 0, lo, hi), -1.5)
        if lev == 2:
            mm("ua", tl, [(I("im16k"), S("r16", lo, hi)), (I("im1"), S("h2", lo, hi))], True, False)
            mm("ub", tl, [(I("i1"), S("d16", lo, hi))] + combo(lo, hi, [0.25] * 4), False, False)
        first = [] if lev == 2 else [(I("i16k"), S("h1", lo, hi))]
        if mode == "D":
            gat("ug" + n, t2, win, lst(ul, 1, lo, hi))
            gop("uc" + n, t, win, lst(ul, 2, lo, hi), t, ALU.add)
            gop("uc" + n, t2, win, lst(ul, 3, lo, hi), t2, ALU.add)
            mm("um" + n, tl, first + [(I("fq"), t)], lev == 1, False)
            mm("um" + n, tl, [(I("fq"), t2)] + rnd, False, True)
        else:
            for j in (1, 2, 3):
                gop("uc" + n, t, win, lst(ul, j, lo, hi), t, ALU.add)
            mm("um" + n, tl, first + [(I("fq"), t)] + rnd, lev == 1, True)
        return tl

    tl = tile(GH)
    mm("wa", tl, [(I("fm16k"), S("hh", V, W)), (I("i16k"), S("x16", V, W)), (I("i1"), S("x16", V, W))], True, False)
    mm("wg", tl, [(I("f1"), S("w2", V, W))], False, True)
    lin("w1g", S("xw2", V, W), tl, 1.0, 0.0)
    for (lo, hi), mode in zip(T4, C["u2"]):
        lin("w1", S("xw2", lo, hi), undo(2, S("w2", 0, W), lo, hi, mode), 1.0, 0.0)
    for (lo, hi), mode in zip(T4, C["u1"]):
        y, tl = S("z2", 2048 + lo, 2048 + hi), undo(1, S("xw2", 0, W), lo, hi, mode)
        if lo in C["yv"]:
            ts("y", y, tl, MAGIC, MAGIC, ALU.add, ALU.subtract)
        else:
            lin("y", y, tl, 1.0, 0.0)
        dma("st_x", ("yx", lo, hi), y, 512 * (hi - lo))
    return ops


def arrange(ops):
    at, seen, calls = {}, {}, {}
    for k, o in enumerate(ops):
        seen[o["name"]] = seen.get(o["name"], -1) + 1
        at["%s.%d" % (o["name"], seen[o["name"]])] = at[o["name"]] = k
        for t in o["tiles"]:
            calls.setdefault(t, []).append(k)
    seq, eng, extra, idle = [], {}, {}, [(b, None) for b in range(8)]
    for x in ORDER.split():
        name, _, e = x.partition("/")
        k = at[name]
        seq.append(k)
        eng[k] = e or list(ops[k]["impl"])[0]
        for t in ops[k]["tiles"]:
            if calls[t][0] == k:
                BANK[t], last = idle.pop(0)
                if last is not None:
                    extra[k] = last
        for t in sorted(ops[k]["tiles"], key=lambda t: calls[t][0]):
            if calls[t][-1] == k:
                idle.append((BANK[t], k))
    assert sorted(seq) == list(range(len(ops)))
    return {"eng": eng, "seq": seq, "extra": extra, "order": {e: [k for k in seq if eng[k] == e] for e in "vapgsx"}}


def plan(ops, sc):
    eng, order = sc["eng"], sc["order"]
    pos = {k: i for e in order for i, k in enumerate(order[e])}
    keep, marked, count = {e: [] for e in order}, set(), {}
    for e in order:
        seen = {}
        for k in order[e]:
            last, deps = {}, set(ops[k]["deps"])
            if k in sc["extra"]:
                deps.add(sc["extra"][k])
            for j in deps:
                if e == "x" or ops[j].get("send") or (e == "p" and eng[j] == "p"):
                    continue
                key = ops[j].get("sem") or eng[j]
                if pos[j] > seen.get(key, -1) and (key not in last or pos[j] > pos[last[key]]):
                    last[key] = j
            for key, j in last.items():
                seen[key] = pos[j]
                marked.add(j)
            keep[e].append((k, sorted(last.values())))
    for e in order:
        c = 0
        for k in order[e]:
            if ops[k].get("sem"):
                count[k] = (ops[k]["sem"], 16)
            elif k in marked:
                c += 1
                count[k] = ("e" + e, c)
    return keep, count


CACHE = {}


def program():
    if "p" not in CACHE:
        ops = build(CFG)
        sc = arrange(ops)
        CACHE["p"] = (ops, sc) + plan(ops, sc)
    return CACHE["p"]


def masks(core, peers, topo):
    lists = [topo.engines(core, p) for p in peers]
    few = min(len(x) for x in lists)
    narrow = [i for i, x in enumerate(lists) if len(x) == few]
    out, used = {}, set()
    for grp in (narrow, [i for i in range(len(peers)) if i not in narrow]):
        for a, i in enumerate(grp):
            av = [e for e in lists[i] if e not in used]
            k = len(av) // (len(grp) - a)
            while k & (k - 1):
                k -= 1
            out[i] = av[:k]
            used |= set(av[:k])
    return [sum(1 << e for e in out[i]) for i in range(len(peers))], [len(out[i]) for i in range(len(peers))]


def rank_program(g, core, T, topo):
    rank = T.rank_of(core)
    if rank is None:
        return
    ops, sc, keep, count = program()
    N = len(T.cores)
    queue = {"v": g.vector, "a": g.scalar, "p": g.tensor, "g": g, "s": g.sync}

    def peers(r, sign):
        return [T.cores[(r + sign * d) % N] for d in range(1, N)]
    arrive = {}
    for o in ops:
        if o.get("send"):
            k, sign = o["impl"]["g"][2][0], o["impl"]["g"][2][4]
            froms = [(rank - sign * d) % N for d in range(1, N)]
            arrive["ar%d" % k] = sum(masks(T.cores[r], peers(r, sign), topo)[1][d] for d, r in enumerate(froms))
    sent = 0
    for e in "sagvp":
        q = queue[e]
        for k, waits in keep[e]:
            for j in waits:
                s, c = count[j]
                q.wait_ge(T.sem[s], arrive.get(s, c))
            f = ops[k]["impl"][e][2]
            if ops[k].get("send"):
                x, src, dst, off, sign = f
                ps = peers(rank, sign)
                mk, ne = masks(core, ps, topo)
                trs = []
                for d, p in enumerate(ps):
                    rid, pid = topo.addr(p, core)
                    trs.append(RemoteDMATransfer(dst_ids=[DstId(rid=rid, pnc=pid)], dma_engine_mask=mk[d], remote_sem=T.sem["ar%d" % x],
                                                 src=T[src][:, NB * d:NB * d + NB], dst=T[dst][:, off + NB * d:off + NB * d + NB]))
                q.remote_dma_fused(trs, local_sem=T.sem.loc)
                sent += sum(ne)
                continue
            ins = f(q, T)
            if k in count:
                ins.then_inc(T.sem[count[k][0]], 16 if ops[k].get("sem") else 1)
        if e == "g":
            q.wait_ge(T.sem.loc, sent)
        if e == "s":
            for o in ops:
                if o.get("final"):
                    q.wait_ge(T.sem[o["sem"]], 16)
